import numpy as np, ml_dtypes
CORES = [66,74,82,90,194,202,210,218]
N = 8
BF = ml_dtypes.bfloat16
V, P, B, C, RO, LG = 1024, 192, 8, 32, 3, 3
PAR = np.array([bin(i).count("1") % 2 for i in range(N)]).reshape(N, 1)
GRP = np.arange(8).reshape(1, 8)
def base(rng):
    nbr = rng.integers(0, V, (8, 16, V)); w = rng.integers(100, 256, (8, 16, V)); b = rng.integers(2 ** 12, 2 ** 19, (8, 16, 1))
    return nbr, w, b, b + rng.integers(0, 100, (N, 8, 16, V))
def stir(rng, x, up, down):
    hi = rng.random((N, 8, V)) < up; lo = (rng.random((N, 8, V)) < down) & ~hi
    m = rng.random(x.shape) < rng.random((N, 8, 1, V))
    a = np.exp2(6 + 13 * rng.random(x.shape)).astype(np.int64); d = np.exp2(12 * rng.random(x.shape)).astype(np.int64)
    x = np.where(hi[:, :, None, :] & m, np.minimum(x + a, 2 ** 20 - 1), x)
    return np.where(lo[:, :, None, :] & m, np.maximum(x - d, 0), x), hi
def names(rng, hi):
    o = np.argsort(rng.random((N, 8, V)) - hi, axis=-1); h = np.add.reduce(hi.astype(np.int64), axis=-1)[:, :, None]
    a = np.take_along_axis(o, (rng.random((N, 8, 16 * P)) * h).astype(np.int64), -1)
    return np.where(rng.random(a.shape) < 0.5, a, rng.integers(0, V, a.shape)).reshape(N, 8, 16, P)
def heights(rng):
    e = rng.choice(np.array([0.1, 0.25, 0.4, 0.6]), (N, 8, 1))
    return np.where(rng.random((N, 8, P)) < e, 0, rng.integers(1, 17, (N, 8, P)))
def pack(nbr, w, x, st, n):
    st = np.where(np.arange(16)[:, None] < n[:, :, None, :], st, 0)
    return {"nb": np.tile(nbr.reshape(1, 128, V), (N, 1, 1)).astype(np.int32), "ln": np.tile(w.reshape(1, 128, V), (N, 1, 1)).astype(np.float32).astype(BF),
            "lab": np.ascontiguousarray(x.reshape(N, 128, V)).astype(np.int32), "stk": np.ascontiguousarray(st.reshape(N, 128, P)).astype(np.int32), "cnt": n.astype(np.int32)}
def setup_inputs(rng):
    nbr, w, b, x = base(rng)
    x, hi = stir(rng, x, rng.choice(np.array([0.02, 0.04, 0.08, 0.16]), (N, 8, 1)), rng.choice(np.array([0.0, 0.001, 0.004]), (N, 8, 1)))
    return pack(nbr, w, x, names(rng, hi), heights(rng))
def setup_inputs_spread(rng):
    nbr, w, b, x = base(rng)
    nbr[1::2] = (V * rng.random((4, 16, V)) ** 3).astype(np.int64); w[1::2] = np.exp2(8 * rng.random((4, 16, V))).astype(np.int64)
    b = np.minimum(np.exp2(20 * rng.random((8, 16, 1))).astype(np.int64), 2 ** 20 - 5000)
    x, hi = stir(rng, b + rng.integers(0, 100, x.shape), 0.06, 0.002)
    x[:, 1::2] = np.minimum((np.exp2(20 * rng.random((N, 4, 1, V))) * rng.random((N, 4, 16, V))).astype(np.int64), 2 ** 20 - 1)
    return pack(nbr, w, x, names(rng, hi), heights(rng))
def setup_inputs_ends(rng):
    e = np.array([0, V - 1])
    nbr = np.where(rng.random((8, 16, V)) < 0.75, rng.choice(e, (8, 16, V)), rng.integers(0, V, (8, 16, V)))
    w = rng.choice(np.array([1, 255]), (8, 16, V))
    k = rng.random((N, 8, 1, V)); x = (2 ** 20 - 1) * np.where(k < 0.7, 1, np.where(k < 0.8, 0, rng.integers(0, 2, (N, 8, 16, V))))
    x[..., e] = (2 ** 20 - 1) * rng.integers(0, 2, (N, 8, 16, 2))
    full = rng.random((N, 8, P)) < rng.choice(np.array([0.3, 0.5, 0.7]), (N, 8, 1))
    n = np.where(rng.random((N, 8, P)) < 0.8, 16 * full, rng.choice(np.array([1, 2, B + 1, B + 2, 15]), (N, 8, P)))
    st = np.where(rng.random((N, 8, 16, P)) < 0.75, rng.choice(e, (N, 8, 16, P)), rng.integers(0, V, (N, 8, 16, P)))
    n[N - 1, 7, P - 1] = 16; st[N - 1, 7, 15, P - 1] = V - 1; n[0, 7, P - 1] = 0; n[0, 0, 0] = 16; st[0, 0, 15, 0] = 0
    return pack(nbr, w, x, st, n)
def setup_inputs_corners(rng):
    nbr, w, b, x = base(rng); v = np.arange(V)
    nbr[1] = v; nbr[2] = rng.choice(np.array([0, V - 1]), (16, V)); nbr[3] = (v + 1) % V; nbr[4] = np.where(rng.random((16, V)) < 0.5, v, V - 1 - v)
    y, hi = stir(rng, x, 0.05, 0.002); x[:, 6:] = y[:, 6:]
    w[0] = rng.choice(np.array([1, 255]), (16, V)); x[:, 0] = b[0] + rng.integers(0, 2, (N, 16, V))
    w[5] = 255; x[:, 5] = 255 * rng.integers(0, 2, (N, 16, V))
    sn = rng.choice(np.array([0, 1, C - 1, C, C + 1, P - C - 1]), (N, 8)); em = rng.choice(np.array([0, 1, C - 1, C, C + 1]), (N, 8))
    sn[0] = (C, C + 1, C, C - 1, 0, C + 1, 1, C); em[1] = (C, C, C + 1, C + 1, C + 1, 0, C, 1)
    sn[N - 1] = (1, P - C - 1, 0, C, C + 1, C - 1, C, C); em[N - 2] = (C, C, C, C - 1, C, C, C, C + 1)
    pos = np.argsort(rng.random((N, 8, P)), axis=-1); sn = sn[:, :, None]; em = em[:, :, None]
    n = np.where(pos < sn, rng.choice(np.array([B + 2, 15, 16]), pos.shape), np.where(pos < sn + em, rng.integers(0, 2, pos.shape), rng.choice(np.array([2, B, B + 1]), pos.shape)))
    return pack(nbr, w, x, names(rng, hi), n)
def setup_inputs_crowd(rng):
    nbr, w, b, x = base(rng); c = rng.integers(1, V - 1, 8); c[0] = 0; c[7] = V - 1
    full = (PAR + GRP) % 2 == 0
    nbr[0:2, :8] = rng.choice(np.array([5, 6, V - 2]), (2, 8, V)); nbr[:, 15] = c[:, None]
    n = np.where(full, 16, 0)[:, :, None] * np.ones((1, 1, P), np.int64)
    st = np.tile(c.reshape(1, 8, 1, 1), (N, 1, 16, P))
    st[:, 3::4] = rng.integers(0, V, (N, 2, 16, 1))
    for q in range(8):
        u = int(c[q]); a = nbr[q, :, u].copy(); a = np.where(a == u, (u + 1) % V, a)
        if q % 2 == 1: a[15] = u
        nbr[q, :, u] = a
        if q % 4 == 2: st[:, q] = rng.choice(np.array([u, 0, V - 1]), (N, 16, P))
        for r in range(N):
            if q % 4 == 1: st[r, q, :, int(rng.integers(0, P))] = rng.integers(0, V, 16)
            if full[r, q] or q >= 4: x[r, q, :, u] = 0
            if q >= 4: n[r, q, int(rng.integers(0, P))] = 0 if full[r, q] else 1
    return pack(nbr, w, x, st, n)
def setup_inputs_calm(rng):
    nbr, w, b, x = base(rng); w = rng.choice(np.array([1, 255]), w.shape)
    b = rng.integers(2 ** 19, 2 ** 20 - 3, b.shape); b[2:4] = 2 ** 20 - 2; b[6:8] = 2 ** 20 - 3; x = b + rng.integers(0, 2, x.shape)
    x[:, 4:] = np.where(rng.random((N, 4, 16, V)) < 0.0005, b[4:] + 2, x[:, 4:])
    r = np.arange(N).reshape(N, 1)
    big = (np.where(GRP % 4 == 2, 0, np.where(GRP % 4 == 3, 1, (PAR + GRP) % 2)) == 1)[:, :, None]
    h = ((r + GRP + rng.integers(0, 4)) % 4)[:, :, None]; few = ((3 * r + GRP + rng.integers(0, 4)) % 4)[:, :, None]
    pos = np.argsort(rng.random((N, 8, P)), axis=-1)
    n = np.where(pos < few, np.where(big, RO, B + 1 + RO), np.where(big, B + RO + rng.integers(0, 2, pos.shape), h + RO - 1))
    return pack(nbr, w, x, rng.integers(0, V, (N, 8, 16, P)), n)
def check_inputs(d):
    bad = []
    for k, lo, hi in (("nb", 0, V - 1), ("ln", 1, 255), ("lab", 0, 2 ** 20 - 1), ("stk", 0, V - 1), ("cnt", 0, 16)):
        a = np.asarray(d[k]).astype(np.float64)
        if not (np.min(a) >= lo and np.max(a) <= hi): bad.append("range of " + k)
        if k == "ln" and not np.all(a == np.floor(a)): bad.append("whole numbers in ln")
        if k in ("nb", "ln") and not np.all(a == a[:1]): bad.append(k + " alike on all ranks")
    s = np.asarray(d["stk"]).reshape(N, 8, 16, P); n = np.asarray(d["cnt"]).reshape(N, 8, 1, P)
    if np.any((np.arange(16)[:, None] >= n) & (s != 0)): bad.append("zeros in the empty slots of stk")
    return bad
def reference(nb, ln, lab, stk, cnt):
    nbr = nb.astype(np.int64).reshape(N, 8, 16, V); w = ln.astype(np.float32).astype(np.int64).reshape(N, 8, 16, V)
    x = lab.astype(np.int64).reshape(N, 8, 16, V); st = stk.astype(np.int64).reshape(N, 8, 16, P); n = cnt.astype(np.int64).reshape(N, 8, P)
    for t in range(RO):
        live = n > 0
        v = np.take_along_axis(st, np.maximum(n - 1, 0)[:, :, None, :], 2)
        k = np.take_along_axis(nbr, v, 3)
        kk = np.ascontiguousarray(k.transpose(0, 1, 3, 2)).reshape(N, 8, 1, 16 * P)
        xk = np.take_along_axis(x, kk, 3).reshape(N, 8, 16, P, 16); wk = np.take_along_axis(w, kk, 3).reshape(N, 8, 16, P, 16)
        y = np.minimum(np.take_along_axis(x, v, 3), np.min(xk, axis=4) + np.take_along_axis(w, v, 3))
        hit = np.any(xk > y[..., None] + wk, axis=2) & live[..., None]
        a, g, l = np.nonzero(live); x[a, g, :, v[a, g, 0, l]] = y[a, g, :, l]
        n = n - live.astype(np.int64); st = np.where(np.arange(16)[:, None] < n[:, :, None, :], st, 0)
        rank = np.add.accumulate(hit.astype(np.int64), axis=3); slot = n[..., None] + rank - 1
        a, g, l, i = np.nonzero(hit & (slot < 16)); st[a, g, slot[a, g, l, i], l] = k[a, g, i, l]
        n = np.minimum(n + rank[..., 15], 16)
        x2, st2, n2 = x.copy(), st.copy(), n.copy()
        for r in range(N):
            q = r ^ (1 << (t % LG))
            for g in range(8):
                give = np.nonzero(n[r, g] > B)[0]; get = np.nonzero(n[q, g] == 0)[0]
                m = min(len(give), len(get), C); give, get = give[:m], get[:m]
                s = st[r, g]; e = s[:B][:, give]
                st2[r, g][:, give] = np.concatenate([s[B:][:, give], np.zeros((B, m), np.int64)]); n2[r, g][give] = n[r, g][give] - B
                st2[q, g][:B, get] = e; n2[q, g][get] = B
                u = e.reshape(-1); x2[q, g][:, u] = np.minimum(x[q, g][:, u], x[r, g][:, u])
        x, st, n = x2, st2, n2
    return {"ylab": x.reshape(N, 128, V).astype(np.float32), "ystk": st.reshape(N, 128, P).astype(np.float32), "ycnt": n.astype(np.float32)}

@@ -1,0 +1,606 @@
+import numpy as np
+from concourse.mybir import AluOpType as Op, ActivationFunctionType as Fn
+
+V, P, STEPS = 1024, 192, 3
+BIG = float(2 ** 21)
+LOSE = 1040
+XSHARE = 40
+PEL = {128: "pq"}
+QA = ()
+HA = True
+CHUNKS = ((0, 64), (64, 128), (128, 192))
+CYC, GATH, SCAT, PEC = np.array([0.9, 1.04, 1.2]), np.array([1.15, 1.56, 2.0]), np.array([2.2, 3.8, 5.4]), np.array([0.45, 0.6, 0.9])
+HOP, FAR, LINK, ISSUE = np.array([80.0, 120.0, 200.0]), np.array([1500.0, 2000.0, 3000.0]), np.array([120.0, 80.0, 50.0]), np.array([200.0, 300.0, 500.0])
+DMA, SLACK, TRIES, NOISE, SEED = 2000.0, 60.0, 150, 1500.0, 0
+ORDER = []
+f32, bf, f16, i32, u16 = "float32", "bfloat16", "float16", "int32", "uint16"
+
+
+def _scratch():
+    s = {}
+
+    def sb(dt, **k):
+        for n, w in k.items():
+            s[n] = ("sbuf", [128, w], dt)
+    sb(i32, nbw=1032, labi=1024, stki=192, cnti=192, pi=2)
+    sb(f32, X=1072, D=1024, XK=3072, MS=3072, DK=3072, ST=256, Kf=192, SC=192, Zt=192, Z=192, LS=200,
+       CC=32, TA=80, k16=80, jr=16, jf=16, vf=16, tp=16, tq=16, up=16, uq=16, LA=4, L4=4, Lp=4, t2=32, NF=16, tS=16, tE=16,
+       MN=256, oj=16, dj=16, I32=128, D32=128, Sh32=128, GV=32, c4=4)
+    sb(bf, W=1040, N=256, U=192, mk=192, C0=192, C1=192, hit=192, CM=3072, fS=192, fE=192, cS=192, cE=192, junk=384,
+       E1=192, E2=192, AB=512, AM=512, WK=3072, RB=1024, RC=512, RZ=192, ones=128, kk=128, ar=192, xr=160, OD=192, TRI=512, key=64, cntb=192,
+       ND=64 * STEPS, G8=128, GT=8, Ob=128, I=128, nI=128, kI=128, nkI=128, kOb=128, LP=128, Dm=128, kD=128, nkD=128, Sh=128,
+       Bz0=160, Bz1=160, Bd0=144, Bd1=144, Sel=2048)
+    sb(f16, TM=192, Q=4 * 192, WN=16 * 192, NX=64)
+    sb(u16, VU=12, VS=24, KU=192, SU=2, NU=16, CU=4, O4=4, JU=16, JG=16)
+    for t in range(STEPS):
+        sb(f32, **{"m1s%d" % t: 52, "m1r%d" % t: 88, "m2s%d" % t: 256, "m2r%d" % t: 256, "m3s%d" % t: 16, "m3r%d" % t: 16})
+    for n in ("pz", "ph", "pp", "pu"):
+        s[n] = ("psum", [128, 512], f32)
+    s["pw"] = ("psum", [128, 1024], f32)
+    s["pq"] = ("psum", [128, 1024], f32)
+    return s
+
+
+SCRATCH = _scratch()
+SEMAPHORES = (["cv", "ca", "cp", "cg", "sent", "l_stk", "l_cnt", "l_nb", "l_lab", "l_ln", "o_lab", "o_stk", "o_cnt"]
+              + ["r%d_%d" % (k, t) for k in (1, 2, 3) for t in range(STEPS)])
+
+
+def rank_program(g, core, T, topo):
+    rank = T.rank_of(core)
+    if rank is None:
+        return
+    ops = []
+
+    def v(name, lo=0, hi=None, step=1, rows=128):
+        if name in ("pl", "pf"):
+            name, lo, hi = ("pq", lo, hi) if name == "pl" else ("pq", 512 + lo, 512 + hi)
+        t = T[name]
+        hi = t.shape[1] if hi is None else hi
+        ap = t[0:rows, lo:hi] if step == 1 else t[0:rows, lo:hi:step]
+        return (ap, [(name, lo, hi)], len(range(lo, hi, step)), SCRATCH[name][2] in (bf, f16, u16), SCRATCH[name][0] == "psum", False)
+
+    def col(name, k):
+        return v(name, k, k + 1)
+
+    def ind(win, off):
+        return (win[0].indirect(off[0]), win[1] + off[1], 16 * off[2], False, False, True)
+
+    def sc(x):
+        return x[0] if isinstance(x, tuple) else x
+
+    def cost(q, o, ins, two):
+        if q == "p":
+            return max(64, ins[1][2]) * PEC * (1 if ins[0][3] else 4)
+        if q == "g":
+            return 170 + 2 * o[2] * CYC
+        full = [x for x in ins if isinstance(x, tuple)][:2 if two else 1]
+        if o[5]:
+            return 50 + o[2] * SCAT * CYC
+        if full and full[0][5]:
+            return 60 + o[2] * GATH * CYC
+        k = 1.0
+        if two == 1:
+            k = 1.0 if any(x[4] for x in full) else 2.0
+        elif q == "v" and o[3] and all(x[3] for x in full):
+            k = 0.5
+        return max(64, o[2] * k) * CYC + (60 if q == "a" else 0)
+
+    def add(q, call, out, ins, sem=None, ext=(), two=0, dur=None, lat=HOP):
+        wr = []
+        rd = []
+        for o in out:
+            wr += o[1][:1]
+            rd += o[1][1:]
+        for x in ins:
+            if isinstance(x, tuple):
+                rd += x[1]
+        if dur is None:
+            dur = cost(q, out[0], ins, two)
+        ops.append((q, call, rd, wr, sem, list(ext), dur + np.zeros(3), lat + np.zeros(3)))
+
+    def cp(o, a):
+        add("v", lambda: g.vector.tensor_copy(o[0], a[0]), [o], [a])
+
+    def tt(o, a, b, op, ext=()):
+        add("v", lambda: g.vector.tensor_tensor(o[0], a[0], b[0], op), [o], [a, b], ext=ext, two=1)
+
+    def ts(o, a, s1, op0, s2=None, op1=None, ext=()):
+        if op1 is None:
+            add("v", lambda: g.vector.tensor_scalar(o[0], a[0], sc(s1), None, op0), [o], [a, s1], ext=ext)
+        else:
+            add("v", lambda: g.vector.tensor_scalar(o[0], a[0], sc(s1), sc(s2), op0, op1), [o], [a, s1, s2], ext=ext)
+
+    def scan(o, a, b, op0, op1):
+        add("v", lambda: g.vector.tensor_tensor_scan(o[0], a[0], b[0], 0.0, op0, op1), [o], [a, b], two=2)
+
+    def ms(o, c):
+        add("v", lambda: g.vector.memset(o[0], c), [o], [])
+
+    def act(o, a, fn=Fn.Copy, bias=None, scale=None, acc=None):
+        kw = {}
+        if bias is not None:
+            kw["bias"] = sc(bias)
+        if scale is not None:
+            kw["scale"] = sc(scale)
+        if acc is not None:
+            kw["accum_out"] = acc[0]
+        add("a", lambda: g.scalar.activation(o[0], a[0], fn, **kw), [o] + ([acc] if acc else []), [a, bias, scale])
+
+    def mm(o, l, r, start=False, stop=False):
+        add("p", lambda: g.tensor.matmul(o[0], l[0], r[0], start, stop), [o], [l, r])
+
+    def iota(o, pat, base=0, cm=0):
+        if o[1][0][0] == "pi":
+            add("g", lambda: g.iota(o[0], pat, base, cm), [o], [])
+        else:
+            add("g", lambda: g.iota(o[0], pat, base, cm, allow_small_or_imprecise_dtypes=True), [o], [])
+
+    def sel(o, a, pat, op, base, cm, fill=0.0):
+        add("g", lambda: g.affine_select(o[0], a[0], pat, op, fill, base, cm), [o], [a])
+
+    def dma(q, o, a, sem, lat):
+        e = g.sync if q == "s" else g.scalar
+        add(q, lambda: e.dma_start(o[0], a[0]), [o], [a], sem=sem, dur=60.0, lat=lat)
+
+    sent = [0]
+    sender = {}
+
+    def send(src, dst, sem, peer):
+        rid, pid = topo.addr(peer, core)
+        mask = topo.mask(core, peer)
+        sent[0] += len(topo.engines(core, peer))
+        add("g", lambda: g.remote_dma(dst[0], src[0], T.sem[sem], T.sem.sent, pid, rid, mask), [], [src], sem="sent",
+            dur=ISSUE, lat=FAR + 512 * src[2] / LINK)
+        sender[sem] = len(ops) - 1
+
+    def hbm(t):
+        return (t[:], [])
+
+    dma("s", v("stki"), hbm(T.stk), "l_stk", DMA + 400)
+    dma("a", v("cnti", rows=8), hbm(T.cnt), "l_cnt", DMA)
+    dma("s", v("labi"), hbm(T.lab), "l_lab", DMA + 2400)
+    dma("s", v("nbw", 0, V), hbm(T.nb), "l_nb", DMA + 4400)
+    dma("s", v("W", 0, V), hbm(T.ln), "l_ln", DMA + 5400)
+
+    ms(v("ones"), 1.0)
+    iota(col("pi", 0), [[0, 1]], 0, 1)
+    iota(v("ar"), [[0, 12], [1, 16]])
+    sel(v("G8"), v("ones"), [[1, 8], [0, 16]], Op.is_equal, 0, -1)
+    sel(v("Ob"), v("ones"), [[-16, 8], [0, 16]], Op.is_ge, 0, 1)
+    sel(v("Ob"), v("Ob"), [[16, 8], [0, 16]], Op.is_ge, 15, -1)
+    sel(v("I"), v("ones"), [[-1, 128]], Op.is_equal, 0, 1)
+    iota(v("k16"), [[16, 80]])
+    iota(v("xr"), [[1, 160]])
+    ms(v("kk"), 1024.0)
+    ms(v("RB"), 0.0)
+    ms(v("RZ"), 1.0)
+    ms(v("ST", P), 0.0)
+    ms(v("N", P), 0.0)
+    ms(v("LS", P), 0.0)
+    ms(v("ND"), 8.0)
+    ms(v("X", V), BIG)
+    ms(v("W", V), BIG)
+    ms(v("nbw", V), 0)
+    ms(v("RB", 0, V, 16), 2 * BIG)
+    ms(v("RZ", 0, P, 16), 0.0)
+    ms(v("RC"), 0.0)
+    ms(v("RC", 0, 512, 32), 2 * BIG)
+    a_i = col("pi", 1)
+    ts(a_i, col("pi", 0), 15, Op.bitwise_and)
+    cA, cA1, cN1, cN2, cM0, cM1, cBF, cBL, cM1k, cG15, cG14, cJ = [col("CC", k) for k in range(12)]
+    cB16, cG, cK0, cK1, cB8 = [col("CC", k) for k in range(20, 25)]
+    cp(cA, a_i)
+    ts(cA1, a_i, 1.0, Op.add)
+    ts(cN1, a_i, -1.0, Op.mult, -1.0, Op.add)
+    ts(cN2, a_i, -1.0, Op.mult, -2.0, Op.add)
+    ts(cM0, a_i, 8.0, Op.is_lt)
+    ts(cM1, a_i, 8.0, Op.is_ge)
+    ts(cM1k, a_i, 8.0, Op.is_ge, -1024.0, Op.mult)
+    ts(cB16, a_i, 8.0, Op.is_ge, 16.0, Op.mult)
+    ts(cB8, a_i, 8.0, Op.is_ge, 8.0, Op.mult)
+    tt(cG, col("pi", 0), a_i, Op.subtract)
+    ts(v("OD"), v("ar"), cA, Op.not_equal, 4096.0, Op.mult)
+    ts(col("pi", 0), a_i, 3, Op.bitwise_and)
+    ts(cG15, cG, 15.0, Op.add)
+    ts(cG14, cG, 14.0, Op.add)
+    ts(cJ, cB16, 1.0, Op.add)
+    ts(cK0, cA, cB8, Op.add)
+    ts(cK1, cA, cB8, Op.add, 8.0, Op.add)
+    ts(cBF, col("pi", 0), -16384.0, Op.mult, 32768.0, Op.add)
+    ts(cBL, col("pi", 0), -16384.0, Op.mult, 33792.0, Op.add)
+    sel(v("Dm"), v("ones"), [[16, 8], [0, 2], [1, 8]], Op.is_equal, 0, -1)
+    sel(v("LP"), v("kk"), [[-16, 8], [0, 16]], Op.is_ge, 0, 1)
+    sel(v("LP"), v("LP"), [[1, 128]], Op.is_ge, 0, -1)
+    sel(v("LP"), v("LP"), [[1, 128]], Op.not_equal, 0, -1, 33792.0)
+    iota(v("jr"), [[1, 16]])
+    iota(v("dj"), [[0, 8], [16, 2]], LOSE)
+    iota(v("key", 0, 32), [[8, 2], [16, 2], [1, 8]])
+    sel(v("Sh"), v("ones"), [[-16, 8], [-128, 2], [-1, 8]], Op.is_equal, -8, 1)
+    for a in range(16):
+        sel(v("Sel", 128 * a, 128 * a + 128), v("ones"), [[16, 8], [0, 16]], Op.is_equal, a, -1)
+    sel(v("GT"), v("ones", 0, 8), [[16, 8]], Op.is_equal, 0, -1)
+    act(v("I32"), v("I"))
+    act(v("nI"), v("I"), scale=-1.0)
+    act(v("kI"), v("I"), scale=1024.0)
+    act(v("nkI"), v("I"), scale=-1024.0)
+    act(v("kOb"), v("Ob"), scale=1024.0)
+    act(v("D32"), v("Dm"))
+    act(v("Sh32"), v("Sh"))
+    act(v("kD"), v("Dm"), scale=1024.0)
+    act(v("nkD"), v("Dm"), scale=-1024.0)
+    ts(v("TA"), v("k16"), cA, Op.add)
+    ts(v("Bz0"), v("xr"), cG15, Op.is_equal)
+    ts(v("Bz1"), v("xr"), cG14, Op.is_equal)
+    ts(v("CC", 12, 14), v("TA", 0, 2), 0.5, Op.add)
+    ts(v("CC", 14, 16), v("TA", 0, 2), 1.0, Op.add)
+    tt(v("Bd0"), v("Bz0", 0, 144), v("Bz0", 8, 152), Op.add)
+    tt(v("Bd1"), v("Bz1", 0, 144), v("Bz1", 8, 152), Op.add)
+    ts(v("jf"), v("jr"), cJ, Op.add)
+    ts(v("dj"), v("dj"), cA, Op.add)
+    ts(v("TRI", 0, 32), v("key", 0, 32), cK0, Op.is_ge, 4096.0, Op.mult)
+    ts(v("TRI", 32, 64), v("key", 0, 32), cK1, Op.is_ge, 4096.0, Op.mult)
+    for w in (64, 128, 256):
+        act(v("TRI", w, 2 * w), v("TRI", 0, w))
+    pj = v("stki", 0, 2)
+    w0, w1 = v("stki", 4, 6), v("stki", 8, 10)
+
+    def pair_lists():
+        cp(pj, v("TA", 0, 2))
+        ts(w0, pj, 1, Op.logical_shift_right)
+        ts(w1, pj, 1, Op.bitwise_and)
+        cp(v("CU", 2, 4), w0)
+        ts(pj, w0, 14, Op.bitwise_and)
+        tt(v("c4", 0, 2), pj, w1, Op.add)
+        cp(v("CU", 0, 2), v("c4", 0, 2))
+
+    cp(v("cntb", rows=8), v("cnti", rows=8))
+    ts(v("ST", 0, P), v("stki"), -1024.0, Op.add)
+    pair_lists()
+    mm(v("ph", 0, P), v("G8", rows=8), v("cntb", rows=8), True, True)
+    cp(v("N", 0, P), v("ph", 0, P))
+
+    def row(i):
+        o = 15 - i
+        return v("Bz%d" % (o % 2), o - o % 2, o - o % 2 + 128)
+
+    def row2(s):
+        o = 7 - s
+        return v("Bd%d" % (o % 2), o - o % 2, o - o % 2 + 128)
+
+    cLose = col("TA", LOSE // 16)
+    Xw = v("X")
+
+    def top():
+        ts(v("mk"), v("N", 0, P), cA1, Op.is_equal, -1.0, Op.mult)
+        scan(v("TM"), v("ST", 0, P), v("mk"), Op.min, Op.mult)
+        mm(v("pz", 0, P), v("I"), v("OD"), True, False)
+        mm(v("pz", 0, P), v("Ob"), v("TM"), False, True)
+        scan(v("SC"), v("RB", 0, P), v("pz", 0, P), Op.add, Op.min)
+        ts(v("VU"), v("SC", 15, P, 16), -1.0, Op.mult, 1024.0, Op.add)
+        cp(v("KU"), ind(v("nbw"), v("VU")))
+        mm(v("pz", P, 2 * P), v("Ob"), v("TM"), True, True)
+
+    def windows(r):
+        if r in QA:
+            act(v("Q", P * r, P * r + P), v("pp", 0, P), Fn.Identity, bias=-(35840.0 + 4096.0 * r))
+        else:
+            ts(v("Q", P * r, P * r + P), v("pp", 0, P), -(35840.0 + 4096.0 * r), Op.add)
+        for q in range(4):
+            s = 4 * r + q
+            ts(v("WN", P * s, P * s + P), v("Q", P * r, P * r + P), -2048.0 + 1024.0 * q, Op.max, -1024.0 + 1024.0 * q, Op.min)
+            if s == 6:
+                mm(v("pl", 0, P), v("nkD"), v("C1"))
+            if s < 8:
+                mm(v("pl", 0, P), row2(s), v("WN", P * s, P * s + P), False, s == 7)
+
+    top()
+    if len(PEL) < len(CHUNKS):
+        mm(v("pw", 0, 512), v("I"), v("W", 0, 512), True, True)
+        mm(v("pw", 512, V), v("I"), v("W", 512, V), True, True)
+    cp(v("X", 0, V), v("labi"))
+
+    for t in range(STEPS):
+        m = 1 << t
+        peer = T.cores[rank ^ m]
+        ne = len(topo.engines(peer, core))
+        hi = (rank & m) != 0
+        cS0, cE0 = (2, 0) if hi else (0, 2)
+        m1s, m1r, m2s, m2r, m3s, m3r = ["m%d%s%d" % (k, x, t) for k in (1, 2, 3) for x in "sr"]
+        own0, dat0, yr0, ur0 = (56, 24, 4, 8) if hi else (0, 0, 80, 64)
+        gs0, us0, ys0 = (0, 32, 48) if hi else (20, 4, 0)
+        nd0 = 64 * t
+
+        for (l0, l1) in CHUNKS:
+            l2 = min(max(l0, XSHARE), l1)
+            if l2 > l0:
+                cp(v("XK", 16 * l0, 16 * l2), ind(Xw, v("KU", l0, l2)))
+            if l1 > l2:
+                act(v("XK", 16 * l2, 16 * l1), ind(Xw, v("KU", l2, l1)))
+        if len(PEL) < len(CHUNKS):
+            tt(v("D"), v("X", 0, V), v("pw"), Op.subtract)
+        act(v("C0"), v("N", 0, P), Fn.Relu, bias=cN2)
+        for (l0, l1) in CHUNKS:
+            if l0 in PEL:
+                act(v("WK", 16 * l0, 16 * l1), ind(v("W"), v("KU", l0, l1)))
+            else:
+                act(v("DK", 16 * l0, 16 * l1), ind(v("D"), v("KU", l0, l1)))
+        cp(v("Kf"), v("KU"))
+        cuts = sorted(set([0, XSHARE] + [c[1] for c in CHUNKS]))
+        for l0, l1 in zip(cuts[:-1], cuts[1:]):
+            scan(v("MS", 16 * l0, 16 * l1), v("RB", 0, 16 * (l1 - l0)), v("XK", 16 * l0, 16 * l1), Op.add, Op.min)
+        mm(v("pu", 0, P), v("I"), v("N", 0, P), True)
+        mm(v("pu", 0, P), v("Ob"), v("mk"))
+        mm(v("pp", 0, P), v("kI"), v("N", 0, P), True)
+        mm(v("pp", 0, P), v("kOb"), v("mk"))
+        mm(v("pp", 0, P), v("I32"), v("Kf"))
+        tt(v("E1"), v("SC"), v("pz", P, 2 * P), Op.is_equal)
+        scan(v("E2"), v("RZ"), v("E1"), Op.mult, Op.add)
+        act(v("vf", 0, 12), v("SC", 15, P, 16), Fn.Identity, bias=1024.0, scale=-1.0)
+        for (l0, l1) in CHUNKS:
+            vu = v("VU", l0 // 16, l1 // 16)
+            tt(v("Zt", l0, l1), ind(v("W"), vu), v("MS", 16 * l0 + 15, 16 * l1, 16), Op.add)
+            tt(v("Z", l0, l1), ind(Xw, vu), v("Zt", l0, l1), Op.min)
+            if l0 not in PEL:
+                cp(v("pz", l0, l1), v("Z", l0, l1))
+        ts(v("tp", 0, 12), v("E2", 15, P, 16), 2.0, Op.is_ge, cLose, Op.mult)
+        tt(v("tq", 0, 12), v("tp", 0, 12), v("vf", 0, 12), Op.max)
+        cp(v("VS", 0, 24, 2), v("tq", 0, 12))
+        for c in range(12):
+            cp(ind(Xw, v("VS", 2 * c, 2 * c + 1)), v("Z", 16 * c, 16 * c + 16))
+        for (l0, l1) in sorted(CHUNKS, key=lambda c: c[0] not in PEL):
+            if l0 in PEL:
+                for h in (0, 512):
+                    mm(v(PEL[l0], h, h + 512), v("nI"), v("WK", 16 * l0 + h, 16 * l0 + h + 512), True)
+                    mm(v(PEL[l0], h, h + 512), v("I32"), v("XK", 16 * l0 + h, 16 * l0 + h + 512), False, True)
+            for i in range(16):
+                if l0 in PEL:
+                    tt(v("CM", P * i + l0, P * i + l1), v(PEL[l0], i, V, 16), v("Z", l0, l1), Op.is_gt)
+                else:
+                    tt(v("CM", P * i + l0, P * i + l1), v("DK", 16 * l0 + i, 16 * l1, 16), v("pz", l0, l1), Op.is_gt)
+                mm(v("ph", l0, l1), row(i), v("CM", P * i + l0, P * i + l1), i == 0, i == 15)
+        for ps, a32, a1, ak in (("pl", "D32", "Dm", "kD"), ("pf", "I32", "I", "kI")):
+            mm(v(ps, 0, P), v(a32), v("ST", 0, P), True)
+            mm(v(ps, 0, P), v(a1), v("TM"))
+            mm(v(ps, 0, P), v(ak), v("mk"))
+            mm(v(ps, 0, P), v(ak), v("C0"))
+        if HA:
+            act(v("hit"), v("ph", 0, P), Fn.Sign)
+        else:
+            ts(v("hit"), v("ph", 0, P), 0.0, Op.is_gt)
+        mm(v("pp", 0, P), v("LP"), v("hit"), False, True)
+        mm(v("pu", 0, P), v("Ob"), v("hit"), False, True)
+        act(v("U"), v("pu", 0, P))
+        ts(v("fS"), v("U"), 9.0, Op.is_ge)
+        act(v("C1"), v("pu", 0, P), Fn.Relu, bias=cN1)
+        act(v("fE"), v("pu", 0, P), Fn.Relu, bias=1.0, scale=-1.0)
+        scan(v("cS"), v("fS"), v("fS"), Op.add, Op.max)
+        scan(v("cE"), v("fE"), v("fE"), Op.add, Op.max)
+        for k in range(2):
+            act(v("junk", P * k, P * k + P), v("cS"), Fn.Sign, bias=col("CC", 12 + k), scale=-1.0, acc=col("LA", cS0 + k))
+        for r in range(4):
+            windows(r)
+        act(v("LS", 0, P), v("pl", 0, P), Fn.Identity, bias=cBL)
+        mm(v("pf", 0, P), v("nkI"), v("C1"))
+        for s in range(16):
+            mm(v("pf", 0, P), row(s), v("WN", P * s, P * s + P), False, s == 15)
+        ts(v("SU"), v("LA", cS0, cS0 + 2), 0.5, Op.mult, 96.0, Op.add)
+        ts(v(m1s, ys0 + cS0, ys0 + cS0 + 2), v("CC", 14, 16), col("cS", P - 1), Op.subtract, 4096.0, Op.mult)
+        ts(v(m1s, ys0 + cE0, ys0 + cE0 + 2), v("CC", 14, 16), col("cE", P - 1), Op.subtract, 4096.0, Op.mult)
+        act(col("c4", 2), col("cS", P - 1), scale=-4096.0)
+        act(col("c4", 3), col("cE", P - 1), scale=-4096.0)
+        act(v("tS"), v("jf"), Fn.Identity, bias=col("c4", 2), scale=4096.0)
+        act(v("tE"), v("jf"), Fn.Identity, bias=col("c4", 3), scale=4096.0)
+        act(v(m1s, gs0, gs0 + 32), ind(v("LS"), v("SU")), Fn.Identity, bias=-1024.0, scale=cM0)
+        ts(v("t2"), ind(v("LS"), v("SU")), cM1, Op.mult, 1024.0, Op.add)
+        tt(v("NF"), v(m1s, gs0, gs0 + 16), v("t2", 16, 32), Op.add)
+        cp(v("NU"), v("NF"))
+        cp(v("NX"), ind(v("NF"), v("CU")))
+        tt(v(m1s, us0, us0 + 16), v("NF"), v("tS"), Op.max)
+        send(v(m1s), v(m1r, 32, 84) if hi else v(m1r, 4, 56), "r1_%d" % t, peer)
+        act(v(m2s), ind(Xw, v("NU")))
+        send(v(m2s), v(m2r), "r2_%d" % t, peer)
+        for k in range(2):
+            act(v("junk", P * k, P * k + P), v("cE"), Fn.Sign, bias=col("CC", 12 + k), scale=-1.0, acc=col("LA", cE0 + k))
+        mm(v("ph"), v("I"), v("TRI"), True)
+        for a in range(16):
+            mm(v("ph", a, 512, 16), v("Sel", 128 * a, 128 * a + 128), v("NX", 0, 32))
+            mm(v("ph", a, 512, 16), v("nI"), v("NX", 32, 64), False, a == 15)
+        act(v("AB"), v("ph"), Fn.Abs, scale=4096.0)
+        act(v("ST", 0, P), v("pf", 0, P), Fn.Identity, bias=cBF)
+        ts(v("N", 0, P), v("U"), 16.0, Op.min)
+        scan(v("AM"), v("RC"), v("AB"), Op.add, Op.min)
+        tt(v(m3s), v("dj"), v("AM", 31, 512, 32), Op.subtract)
+        send(v(m3s), v(m3r), "r3_%d" % t, peer)
+        act(v("GV"), ind(v("ST"), v("SU")))
+        mm(v("pz", 384, 416), v("Sh32"), v("GV"), True, True)
+        act(v(m1r, own0, own0 + 32), v("pz", 384, 416), Fn.Identity, bias=cM1k)
+        act(v("L4"), v("LA"), Fn.Identity, bias=96.0, scale=0.5)
+        tt(v("Lp"), v("L4"), v(m1s, ys0, ys0 + 4), Op.max)
+        act(v("ND", nd0 + 16 * cS0, nd0 + 16 * cS0 + 32), ind(v("N"), v("SU")), Fn.Identity, bias=-8.0)
+        for k in range(4):
+            ts(col("O4", k), col(m1r, yr0 + k), col("Lp", k), Op.max, col("TA", 12 + k), Op.min, ext=[("r1_%d" % t, ne)])
+        cp(ind(v("N"), v("O4")), v("ND", nd0, nd0 + 64))
+        cp(ind(v("ST"), v("O4")), v(m1r, dat0, dat0 + 64))
+        if t + 1 < STEPS:
+            top()
+        else:
+            act(v("Zt"), v("ST", 0, P), Fn.Identity, bias=1024.0)
+            mm(v("pu", 0, P, rows=8), v("GT"), v("N", 0, P), True, True)
+            act(v("SC", rows=8), v("pu", 0, P, rows=8))
+            dma("s", hbm(T.ystk), v("Zt"), "o_stk", DMA + 400)
+            dma("s", hbm(T.ycnt), v("SC", rows=8), "o_cnt", DMA)
+        tt(v("uq"), v(m1r, ur0, ur0 + 16), v("tE"), Op.max, ext=[("r1_%d" % t, ne)])
+        tt(v("up"), v("uq"), v("dj"), Op.min)
+        cp(v("JG"), v("up"))
+        tt(v("MN"), ind(Xw, v("JG")), v(m2r), Op.min, ext=[("r2_%d" % t, ne)])
+        tt(v("oj"), v(m3r), v("up"), Op.max, ext=[("r3_%d" % t, ne)])
+        cp(v("JU"), v("oj"))
+        for c in range(8):
+            cp(ind(Xw, v("JU", 2 * c, 2 * c + 2)), v("MN", 32 * c, 32 * c + 32))
+    dma("s", hbm(T.ylab), v("X", 0, V), "o_lab", DMA + 2000)
+
+    emit(g, T, ops, sender)
+    g.wait_ge(T.sem.sent, sent[0])
+    for s in ("o_stk", "o_cnt", "o_lab"):
+        g.sync.wait_ge(T.sem[s], 16)
+
+
+def choose(ops, deps):
+    n = len(ops)
+    qs = [o[0] for o in ops]
+    dur = [[float(o[6][m]) for o in ops] for m in range(3)]
+    lat = [[float(o[7][m]) for o in ops] for m in range(3)]
+    covered = [0] * n
+    near = []
+    for j in range(n):
+        mask = 0
+        keep = []
+        for k in sorted(deps[j], reverse=True):
+            if not (mask >> k) & 1 or ops[k][4] is not None:
+                keep.append((k, deps[j][k]))
+            if deps[j][k]:
+                mask |= covered[k]
+        near.append(keep)
+        for k in deps[j]:
+            mask |= covered[k] | (1 << k)
+        covered[j] = mask
+    after = [[] for _ in range(n)]
+    for j in range(n):
+        for k, hard in near[j]:
+            after[k].append((j, hard))
+
+    def tails(order, m):
+        tail = [0.0] * n
+        nxt = {}
+        for j in reversed(order):
+            x = dur[m][j] + lat[m][j]
+            for k, hard in after[j]:
+                x = max(x, dur[m][j] + (lat[m][j] if hard else 0.0) + tail[k])
+            tail[j] = x
+        return tail
+
+    def span(order, m):
+        free = {}
+        end = [0.0] * n
+        last = 0.0
+        for j in order:
+            t0 = free.get(qs[j], 0.0)
+            for k, hard in near[j]:
+                t0 = max(t0, end[k] + (lat[m][k] if hard else 0.0))
+            end[j] = free[qs[j]] = t0 + dur[m][j]
+            last = max(last, end[j] + lat[m][j])
+        return last
+
+    def schedule(prio, m):
+        left = [len(d) for d in near]
+        ready = [j for j in range(n) if left[j] == 0]
+        early = [0.0] * n
+        free = {q: 0.0 for q in "vapgs"}
+        order = []
+        while ready:
+            t0, first = min((max(early[j], free[qs[j]]), j) for j in ready)
+            q = qs[first]
+            j = max((prio[k], -k) for k in ready if qs[k] == q and early[k] <= t0 + SLACK)
+            j = -j[1]
+            t0 = max(early[j], free[q])
+            free[q] = t0 + dur[m][j]
+            ready.remove(j)
+            order.append(j)
+            for k, hard in after[j]:
+                early[k] = max(early[k], free[q] + (lat[m][j] if hard else 0.0))
+                left[k] -= 1
+                if left[k] == 0:
+                    ready.append(k)
+        return order
+
+    rng = np.random.default_rng(SEED)
+    base = np.array(tails(range(n), 1))
+    keys = {}
+    kind = np.array([keys.setdefault((o[0], (o[3] + o[2])[0][0].rstrip("012"), len(o[3])), len(keys)) for o in ops])
+    bump = np.zeros(len(keys))
+    best, score = None, None
+    for it in range(TRIES):
+        trial = bump + (rng.normal(0.0, NOISE, len(keys)) * (rng.random(len(keys)) < 0.05) if it else 0.0)
+        order = schedule((base + trial[kind]).tolist(), 1)
+        s = [span(order, m) for m in range(3)]
+        s = s[0] / 0.8 + s[1] + s[2] / 1.3
+        if score is None or s < score:
+            best, score, bump = order, s, trial
+    return best
+
+
+def emit(g, T, ops, sender):
+    n = len(ops)
+    log = {}
+    deps = []
+    for j, (q, call, rd, wr, sem, ext, dur, lat) in enumerate(ops):
+        d = {}
+        for acc, w in [(x, False) for x in rd] + [(x, True) for x in wr]:
+            name, a, b = acc
+            ps = SCRATCH[name][0] == "psum"
+            lo, hi = (a // 512 * 512, (b + 511) // 512 * 512) if ps else (a, b)
+            for (k, l2, h2, w2, a2, b2) in log.get(name, []):
+                if l2 >= hi or lo >= h2 or k == j:
+                    continue
+                if ops[k][0] != q or ops[k][4] is not None or sem is not None:
+                    if w or w2 or ps:
+                        d[k] = True
+                elif q == "p":
+                    d[k] = False
+                elif a2 < b and a < b2 and (w or w2):
+                    d[k] = True
+            log.setdefault(name, []).append((j, lo, hi, w, a, b))
+        for s, c in ext:
+            d[sender[s]] = True
+        if j in (2, 3, 4):
+            d[0 if j == 2 else j - 1] = None
+        deps.append(d)
+    if not ORDER:
+        ORDER.extend(choose(ops, deps))
+    order = ORDER
+    place = {j: i for i, j in enumerate(order)}
+    assert len(order) == n and all(place[k] < place[j] for j in range(n) for k in deps[j])
+    queues = {"v": g.vector, "a": g.scalar, "p": g.tensor, "g": g, "s": g.sync}
+    counter = {"v": "cv", "a": "ca", "p": "cp", "g": "cg"}
+    seen = {}
+    need = set()
+    waits = {}
+    for j in order:
+        q = ops[j][0]
+        mine = []
+        best = {}
+        for k, hard in deps[j].items():
+            if ops[k][4] is not None:
+                if hard and ops[k][4] != "sent" and (q, ops[k][4]) not in seen:
+                    seen[(q, ops[k][4])] = 16
+                    mine.append((False, ops[k][4], 16))
+            elif hard and place[k] > place.get(best.get(ops[k][0]), -1):
+                best[ops[k][0]] = k
+        for q2, k in best.items():
+            if seen.get((q, q2), -1) < place[k]:
+                seen[(q, q2)] = place[k]
+                need.add(k)
+                mine.append((True, q2, k))
+        for s, c in ops[j][5]:
+            if (q, s) not in seen:
+                seen[(q, s)] = c
+                mine.append((False, s, c))
+        waits[j] = mine
+    count = {}
+    total = {"v": 0, "a": 0, "p": 0, "g": 0}
+    for j in order:
+        q, call, sem = ops[j][0], ops[j][1], ops[j][4]
+        for own, s, c in waits[j]:
+            if own:
+                queues[q].wait_ge(T.sem[counter[s]], count[c])
+            else:
+                queues[q].wait_ge(T.sem[s], c)
+        ins = call()
+        if sem is not None:
+            if sem != "sent":
+                ins.then_inc(T.sem[sem], 16)
+        elif j in need:
+            total[q] += 1
+            count[j] = total[q]
+            ins.then_inc(T.sem[counter[q]], 1)

@@ -4,14 +4,25 @@ from concourse.mybir import AluOpType as Op, ActivationFunctionType as Fn
 V, P, STEPS = 1024, 192, 3
 BIG = float(2 ** 21)
 LOSE = 1040
-XSHARE = 40
-PEL = {128: "pq"}
-QA = ()
-HA = True
 CHUNKS = ((0, 64), (64, 128), (128, 192))
-CYC, GATH, SCAT, PEC = np.array([0.9, 1.04, 1.2]), np.array([1.15, 1.56, 2.0]), np.array([2.2, 3.8, 5.4]), np.array([0.45, 0.6, 0.9])
-HOP, FAR, LINK, ISSUE = np.array([80.0, 120.0, 200.0]), np.array([1500.0, 2000.0, 3000.0]), np.array([120.0, 80.0, 50.0]), np.array([200.0, 300.0, 500.0])
-DMA, SLACK, TRIES, NOISE, SEED = 2000.0, 60.0, 150, 1500.0, 0
+FUSE = 64
+XSHARE = 16
+WCUT, FCUT = 32, 64
+MSPLIT = 8
+LOADS = ("nb", "ln", "lab")
+ALIAS = {"pd": ("pa", 512, 512), "ps": ("pa", 0, 512), "pn": ("ph", 0, 512)}
+CYC = np.array([0.83, 1.1, 1.0, 0.95, 1.15])
+GATH = np.array([1.56, 1.5, 1.2, 2.05, 1.8])
+SCAT = np.array([3.8, 3.8, 5.0, 4.5, 2.2])
+PEC = CYC * np.array([0.5, 0.5, 0.85, 0.5, 0.85])
+HOP = np.array([180.0, 130.0, 230.0, 150.0, 180.0])
+FAR = np.array([900.0, 600.0, 1200.0, 1000.0, 1800.0]) + HOP
+LINK = np.array([216.0, 280.0, 200.0, 200.0, 120.0])
+ISSUE = np.array([450.0, 450.0, 300.0, 450.0, 700.0])
+ROWS = np.array([290.0, 160.0, 500.0, 300.0, 300.0])
+WEIGHT = (1.5, 1.5, 0.5, 1.5, 0.5)
+ACT, DMA, LOAD, SLACK = 90.0, 2000.0, 800.0, 60.0
+TURNS, MOVES, WIDTH, PATIENCE, SEED = 6, 2000, 40, 100, 0
 ORDER = []
 f32, bf, f16, i32, u16 = "float32", "bfloat16", "float16", "int32", "uint16"
 
@@ -23,26 +34,28 @@ def _scratch():
         for n, w in k.items():
             s[n] = ("sbuf", [128, w], dt)
     sb(i32, nbw=1032, labi=1024, stki=192, cnti=192, pi=2)
-    sb(f32, X=1072, D=1024, XK=3072, MS=3072, DK=3072, ST=256, Kf=192, SC=192, Zt=192, Z=192, LS=200,
-       CC=32, TA=80, k16=80, jr=16, jf=16, vf=16, tp=16, tq=16, up=16, uq=16, LA=4, L4=4, Lp=4, t2=32, NF=16, tS=16, tE=16,
-       MN=256, oj=16, dj=16, I32=128, D32=128, Sh32=128, GV=32, c4=4)
-    sb(bf, W=1040, N=256, U=192, mk=192, C0=192, C1=192, hit=192, CM=3072, fS=192, fE=192, cS=192, cE=192, junk=384,
-       E1=192, E2=192, AB=512, AM=512, WK=3072, RB=1024, RC=512, RZ=192, ones=128, kk=128, ar=192, xr=160, OD=192, TRI=512, key=64, cntb=192,
-       ND=64 * STEPS, G8=128, GT=8, Ob=128, I=128, nI=128, kI=128, nkI=128, kOb=128, LP=128, Dm=128, kD=128, nkD=128, Sh=128,
-       Bz0=160, Bz1=160, Bd0=144, Bd1=144, Sel=2048)
-    sb(f16, TM=192, Q=4 * 192, WN=16 * 192, NX=64)
-    sb(u16, VU=12, VS=24, KU=192, SU=2, NU=16, CU=4, O4=4, JU=16, JG=16)
-    for t in range(STEPS):
-        sb(f32, **{"m1s%d" % t: 52, "m1r%d" % t: 88, "m2s%d" % t: 256, "m2r%d" % t: 256, "m3s%d" % t: 16, "m3r%d" % t: 16})
-    for n in ("pz", "ph", "pp", "pu"):
+    sb(f32, XF=1104, XG=1064, D=1024, W4=1024, XK=1024, XL=1024, XM=1024, DK=3072, MS=9248, W3=576, Z3=576, OG=256, ST=256,
+       LS=200, SC=192, out=192, CC=32, TA=80, k16=80, jr=16, JT=16, vf=16, tp=16, tq=16, up=16, uq=16, LA=4, L4=4, Lp=4, NF=16,
+       nt=16, oj=16, dj=16, dl=16, I32=128, Sh32=128, GV=32, c4=2)
+    sb(bf, W=1040, WK=1024, CM=3072, N=256, U=192, mk=192, C0=192, C1=192, hit=192, fS=192, fE=192, cS=192, cE=192, junk=384,
+       E1=192, E2=192, AB=384, AM=384, RB=384, RN=1024, R8=512, RZ=192, ones=192, kk=128, ar=256, xr=160, OD=192, TRI=384,
+       alt=16, cntb=192, ND=64 * STEPS, G8=128, GT=8, Ob=128, I=128, nI=128, kI=128, kOb=128, dB=128, LP=128, Up=128, Lo=128,
+       Hi=128, Sh=128, Bz0=160, Bz1=160, Sel=2048)
+    sb(f16, TM=192, Kh=192, GH=32, Q=4 * 192, WN=16 * 192, NX=24, DR=128)
+    sb(u16, VU=12, VS=24, KU=192, KP=128, SU=2, NU=16, CU=8, O4=4, JU=16, JG=16)
+    ALIAS["X"], ALIAS["XO"] = ("XF", 32, 1072), ("XG", 32, 1024)
+    for n, w in (("m1s", 52), ("m1r", 88), ("m2s", 256), ("m2r", 256), ("m3s", 16), ("m3r", 16)):
+        sb(f32, **{n: w * STEPS})
+        for t in range(STEPS):
+            ALIAS["%s%d" % (n, t)] = (n, w * t, w)
+    for n in ("pz", "ph", "pp", "pu", "pl", "pf"):
         s[n] = ("psum", [128, 512], f32)
-    s["pw"] = ("psum", [128, 1024], f32)
-    s["pq"] = ("psum", [128, 1024], f32)
+    s["pa"] = ("psum", [128, 1024], f32)
     return s
 
 
 SCRATCH = _scratch()
-SEMAPHORES = (["cv", "ca", "cp", "cg", "sent", "l_stk", "l_cnt", "l_nb", "l_lab", "l_ln", "o_lab", "o_stk", "o_cnt"]
+SEMAPHORES = (["cv", "ca", "cp", "cg", "sent", "l_stk", "l_cnt", "l_nb", "l_lab0", "l_lab1", "l_ln", "o_lab", "o_stk", "o_cnt"]
               + ["r%d_%d" % (k, t) for k in (1, 2, 3) for t in range(STEPS)])
 
 
@@ -53,12 +66,15 @@ def rank_program(g, core, T, topo):
     ops = []
 
     def v(name, lo=0, hi=None, step=1, rows=128):
-        if name in ("pl", "pf"):
-            name, lo, hi = ("pq", lo, hi) if name == "pl" else ("pq", 512 + lo, 512 + hi)
+        if name == "Z":
+            name, lo, hi, step = "Z3", 3 * lo + 1, 3 * hi, 3
+        if name in ALIAS:
+            name, at, w = ALIAS[name]
+            lo, hi = at + lo, at + (w if hi is None else hi)
         t = T[name]
         hi = t.shape[1] if hi is None else hi
         ap = t[0:rows, lo:hi] if step == 1 else t[0:rows, lo:hi:step]
-        return (ap, [(name, lo, hi)], len(range(lo, hi, step)), SCRATCH[name][2] in (bf, f16, u16), SCRATCH[name][0] == "psum", False)
+        return (ap, [(name, lo, hi, step)], len(range(lo, hi, step)), SCRATCH[name][2] in (bf, f16, u16), SCRATCH[name][0] == "psum", False)
 
     def col(name, k):
         return v(name, k, k + 1)
@@ -84,7 +100,7 @@ def rank_program(g, core, T, topo):
             k = 1.0 if any(x[4] for x in full) else 2.0
         elif q == "v" and o[3] and all(x[3] for x in full):
             k = 0.5
-        return max(64, o[2] * k) * CYC + (60 if q == "a" else 0)
+        return max(64, o[2] * k) * CYC + (ACT if q == "a" else 0)
 
     def add(q, call, out, ins, sem=None, ext=(), two=0, dur=None, lat=HOP):
         wr = []
@@ -97,10 +113,10 @@ def rank_program(g, core, T, topo):
                 rd += x[1]
         if dur is None:
             dur = cost(q, out[0], ins, two)
-        ops.append((q, call, rd, wr, sem, list(ext), dur + np.zeros(3), lat + np.zeros(3)))
+        ops.append((q, call, rd, wr, sem, list(ext), dur + 0 * CYC, lat + 0 * CYC))
 
-    def cp(o, a):
-        add("v", lambda: g.vector.tensor_copy(o[0], a[0]), [o], [a])
+    def cp(o, a, ext=()):
+        add("v", lambda: g.vector.tensor_copy(o[0], a[0]), [o], [a], ext=ext)
 
     def tt(o, a, b, op, ext=()):
         add("v", lambda: g.vector.tensor_tensor(o[0], a[0], b[0], op), [o], [a, b], ext=ext, two=1)
@@ -111,13 +127,13 @@ def rank_program(g, core, T, topo):
         else:
             add("v", lambda: g.vector.tensor_scalar(o[0], a[0], sc(s1), sc(s2), op0, op1), [o], [a, s1, s2], ext=ext)
 
-    def scan(o, a, b, op0, op1):
-        add("v", lambda: g.vector.tensor_tensor_scan(o[0], a[0], b[0], 0.0, op0, op1), [o], [a, b], two=2)
+    def scan(o, a, b, op0, op1, ext=()):
+        add("v", lambda: g.vector.tensor_tensor_scan(o[0], a[0], b[0], 0.0, op0, op1), [o], [a, b], ext=ext, two=2)
 
     def ms(o, c):
         add("v", lambda: g.vector.memset(o[0], c), [o], [])
 
-    def act(o, a, fn=Fn.Copy, bias=None, scale=None, acc=None):
+    def act(o, a, fn=Fn.Copy, bias=None, scale=None, acc=None, ext=()):
         kw = {}
         if bias is not None:
             kw["bias"] = sc(bias)
@@ -125,7 +141,7 @@ def rank_program(g, core, T, topo):
             kw["scale"] = sc(scale)
         if acc is not None:
             kw["accum_out"] = acc[0]
-        add("a", lambda: g.scalar.activation(o[0], a[0], fn, **kw), [o] + ([acc] if acc else []), [a, bias, scale])
+        add("a", lambda: g.scalar.activation(o[0], a[0], fn, **kw), [o] + ([acc] if acc else []), [a, bias, scale], ext=ext)
 
     def mm(o, l, r, start=False, stop=False):
         add("p", lambda: g.tensor.matmul(o[0], l[0], r[0], start, stop), [o], [l, r])
@@ -151,112 +167,105 @@ def rank_program(g, core, T, topo):
         mask = topo.mask(core, peer)
         sent[0] += len(topo.engines(core, peer))
         add("g", lambda: g.remote_dma(dst[0], src[0], T.sem[sem], T.sem.sent, pid, rid, mask), [], [src], sem="sent",
-            dur=ISSUE, lat=FAR + 512 * src[2] / LINK)
+            dur=ISSUE, lat=0.0)
+        add("d", None, [], [], sem="sent", dur=ROWS + 512 * src[2] / LINK, lat=FAR)
         sender[sem] = len(ops) - 1
 
     def hbm(t):
         return (t[:], [])
 
-    dma("s", v("stki"), hbm(T.stk), "l_stk", DMA + 400)
-    dma("a", v("cnti", rows=8), hbm(T.cnt), "l_cnt", DMA)
-    dma("s", v("labi"), hbm(T.lab), "l_lab", DMA + 2400)
-    dma("s", v("nbw", 0, V), hbm(T.nb), "l_nb", DMA + 4400)
-    dma("s", v("W", 0, V), hbm(T.ln), "l_ln", DMA + 5400)
+    dma("s", v("stki"), hbm(T.stk), "l_stk", DMA)
+    dma("a", v("cnti", rows=8), hbm(T.cnt), "l_cnt", DMA - 400)
+    late = DMA
+    for name in LOADS:
+        if name == "lab":
+            for h in (0, 1):
+                late += LOAD
+                dma("s", v("labi", 512 * h, 512 * h + 512), (T.lab[:, 512 * h:512 * h + 512], []), "l_lab%d" % h, late)
+        elif name == "nb":
+            late += 2 * LOAD
+            dma("s", v("nbw", 0, V), hbm(T.nb), "l_nb", late)
+        else:
+            late += LOAD
+            dma("s", v("W", 0, V), hbm(T.ln), "l_ln", late)
 
+    one = v("ones", 0, 128)
     ms(v("ones"), 1.0)
     iota(col("pi", 0), [[0, 1]], 0, 1)
-    iota(v("ar"), [[0, 12], [1, 16]])
-    sel(v("G8"), v("ones"), [[1, 8], [0, 16]], Op.is_equal, 0, -1)
-    sel(v("Ob"), v("ones"), [[-16, 8], [0, 16]], Op.is_ge, 0, 1)
+    iota(v("ar"), [[0, 16], [1, 16]])
+    sel(v("G8"), one, [[1, 8], [0, 16]], Op.is_equal, 0, -1)
+    sel(v("Ob"), one, [[-16, 8], [0, 16]], Op.is_ge, 0, 1)
     sel(v("Ob"), v("Ob"), [[16, 8], [0, 16]], Op.is_ge, 15, -1)
-    sel(v("I"), v("ones"), [[-1, 128]], Op.is_equal, 0, 1)
+    sel(v("I"), one, [[-1, 128]], Op.is_equal, 0, 1)
     iota(v("k16"), [[16, 80]])
     iota(v("xr"), [[1, 160]])
     ms(v("kk"), 1024.0)
-    ms(v("RB"), 0.0)
-    ms(v("RZ"), 1.0)
+    for name, w, gap, fill, mark in (("RB", 384, 16, 0.0, 2 * BIG), ("RN", V, 16, 0.0, -4096.0), ("RZ", P, 16, 1.0, 0.0),
+                                     ("R8", 512, 8, 0.0, -4096.0), ("alt", 16, 2, -1.0, 0.0)):
+        ms(v(name), fill)
+        ms(v(name, 0, w, gap), mark)
     ms(v("ST", P), 0.0)
     ms(v("N", P), 0.0)
-    ms(v("LS", P), 0.0)
+    ms(v("LS", P), -1024.0)
     ms(v("ND"), 8.0)
-    ms(v("X", V), BIG)
+    ms(v("X", V), -2048.0)
+    ms(v("XF", 0, 32), -2048.0)
+    ms(v("MS", 77, 48 * P + 30, 48), -4096.0)
+    ms(v("W3", 0, 3 * P, 3), -4096.0)
+    ms(v("W3", 2, 3 * P, 3), 0.0)
     ms(v("W", V), BIG)
     ms(v("nbw", V), 0)
-    ms(v("RB", 0, V, 16), 2 * BIG)
-    ms(v("RZ", 0, P, 16), 0.0)
-    ms(v("RC"), 0.0)
-    ms(v("RC", 0, 512, 32), 2 * BIG)
+    ms(v("TRI", 256, 384), 0.0)
     a_i = col("pi", 1)
     ts(a_i, col("pi", 0), 15, Op.bitwise_and)
-    cA, cA1, cN1, cN2, cM0, cM1, cBF, cBL, cM1k, cG15, cG14, cJ = [col("CC", k) for k in range(12)]
-    cB16, cG, cK0, cK1, cB8 = [col("CC", k) for k in range(20, 25)]
+    cA, cA1, cN1, cN2, cM0, cBF, cM1k, cG15, cG14, cJ, cG, cH = [col("CC", k) for k in range(12)]
     cp(cA, a_i)
     ts(cA1, a_i, 1.0, Op.add)
-    ts(cN1, a_i, -1.0, Op.mult, -1.0, Op.add)
+    ts(cN1, a_i, -1024.0, Op.mult, -1024.0, Op.add)
     ts(cN2, a_i, -1.0, Op.mult, -2.0, Op.add)
     ts(cM0, a_i, 8.0, Op.is_lt)
-    ts(cM1, a_i, 8.0, Op.is_ge)
     ts(cM1k, a_i, 8.0, Op.is_ge, -1024.0, Op.mult)
-    ts(cB16, a_i, 8.0, Op.is_ge, 16.0, Op.mult)
-    ts(cB8, a_i, 8.0, Op.is_ge, 8.0, Op.mult)
+    ts(cH, a_i, 8.0, Op.is_lt, -0.5, Op.add)
     tt(cG, col("pi", 0), a_i, Op.subtract)
-    ts(v("OD"), v("ar"), cA, Op.not_equal, 4096.0, Op.mult)
+    ts(v("OD"), v("ar", 0, P), cA, Op.not_equal, 4096.0, Op.mult)
     ts(col("pi", 0), a_i, 3, Op.bitwise_and)
     ts(cG15, cG, 15.0, Op.add)
     ts(cG14, cG, 14.0, Op.add)
-    ts(cJ, cB16, 1.0, Op.add)
-    ts(cK0, cA, cB8, Op.add)
-    ts(cK1, cA, cB8, Op.add, 8.0, Op.add)
+    ts(cJ, cA, 2.0, Op.mult, cH, Op.add)
     ts(cBF, col("pi", 0), -16384.0, Op.mult, 32768.0, Op.add)
-    ts(cBL, col("pi", 0), -16384.0, Op.mult, 33792.0, Op.add)
-    sel(v("Dm"), v("ones"), [[16, 8], [0, 2], [1, 8]], Op.is_equal, 0, -1)
+    ts(v("dB"), v("I"), cBF, Op.mult)
+    for name, base in (("Up", 128), ("Lo", 0), ("Sh", -8), ("Hi", 120)):
+        sel(v(name), one, [[-16, 8], [-128, 2], [-1, 8]], Op.is_equal, base, 1)
     sel(v("LP"), v("kk"), [[-16, 8], [0, 16]], Op.is_ge, 0, 1)
     sel(v("LP"), v("LP"), [[1, 128]], Op.is_ge, 0, -1)
     sel(v("LP"), v("LP"), [[1, 128]], Op.not_equal, 0, -1, 33792.0)
-    iota(v("jr"), [[1, 16]])
-    iota(v("dj"), [[0, 8], [16, 2]], LOSE)
-    iota(v("key", 0, 32), [[8, 2], [16, 2], [1, 8]])
-    sel(v("Sh"), v("ones"), [[-16, 8], [-128, 2], [-1, 8]], Op.is_equal, -8, 1)
+    iota(v("jr"), [[-2, 16]])
+    iota(v("dj"), [[0, 8], [-16, 2]], 16)
+    act(v("nI"), v("I"), scale=-1.0)
     for a in range(16):
-        sel(v("Sel", 128 * a, 128 * a + 128), v("ones"), [[16, 8], [0, 16]], Op.is_equal, a, -1)
+        sel(v("Sel", 128 * a, 128 * a + 128), v("nI"), [[16, 8], [0, 16]], Op.not_equal, a, -1, 1.0)
+        sel(v("Sel", 129 * a, 128 * a + 128, 16), v("Sel", 129 * a, 128 * a + 128, 16), [[16, 8]], Op.not_equal, a, -1)
     sel(v("GT"), v("ones", 0, 8), [[16, 8]], Op.is_equal, 0, -1)
     act(v("I32"), v("I"))
-    act(v("nI"), v("I"), scale=-1.0)
     act(v("kI"), v("I"), scale=1024.0)
-    act(v("nkI"), v("I"), scale=-1024.0)
     act(v("kOb"), v("Ob"), scale=1024.0)
-    act(v("D32"), v("Dm"))
     act(v("Sh32"), v("Sh"))
-    act(v("kD"), v("Dm"), scale=1024.0)
-    act(v("nkD"), v("Dm"), scale=-1024.0)
+    for h in (0, 512):
+        act(v("W4", h, h + 512), v("W", h, h + 512), Fn.Identity, bias=4096.0, scale=1.0 / 1024)
     ts(v("TA"), v("k16"), cA, Op.add)
     ts(v("Bz0"), v("xr"), cG15, Op.is_equal)
     ts(v("Bz1"), v("xr"), cG14, Op.is_equal)
-    ts(v("CC", 12, 14), v("TA", 0, 2), 0.5, Op.add)
-    ts(v("CC", 14, 16), v("TA", 0, 2), 1.0, Op.add)
-    tt(v("Bd0"), v("Bz0", 0, 144), v("Bz0", 8, 152), Op.add)
-    tt(v("Bd1"), v("Bz1", 0, 144), v("Bz1", 8, 152), Op.add)
-    ts(v("jf"), v("jr"), cJ, Op.add)
+    for k in range(2):
+        ts(col("CC", 12 + k), a_i, 2.0, Op.mult, 1.5 - k, Op.add)
+        ts(col("CC", 14 + k), a_i, 2.0, Op.mult, 2.0 - k, Op.add)
+        ts(col("CC", 16 + k), a_i, 4.0, Op.mult, 4.0 - 2 * k, Op.add)
+    ts(v("JT"), v("jr"), cJ, Op.add, 4096.0, Op.mult)
     ts(v("dj"), v("dj"), cA, Op.add)
-    ts(v("TRI", 0, 32), v("key", 0, 32), cK0, Op.is_ge, 4096.0, Op.mult)
-    ts(v("TRI", 32, 64), v("key", 0, 32), cK1, Op.is_ge, 4096.0, Op.mult)
-    for w in (64, 128, 256):
-        act(v("TRI", w, 2 * w), v("TRI", 0, w))
-    pj = v("stki", 0, 2)
-    w0, w1 = v("stki", 4, 6), v("stki", 8, 10)
-
-    def pair_lists():
-        cp(pj, v("TA", 0, 2))
-        ts(w0, pj, 1, Op.logical_shift_right)
-        ts(w1, pj, 1, Op.bitwise_and)
-        cp(v("CU", 2, 4), w0)
-        ts(pj, w0, 14, Op.bitwise_and)
-        tt(v("c4", 0, 2), pj, w1, Op.add)
-        cp(v("CU", 0, 2), v("c4", 0, 2))
+    ts(v("TRI", 0, 256), v("ar"), cA, Op.is_ge, 4096.0, Op.mult)
+    cp(v("CU"), v("xr", 1, 16, 2))
 
     cp(v("cntb", rows=8), v("cnti", rows=8))
     ts(v("ST", 0, P), v("stki"), -1024.0, Op.add)
-    pair_lists()
     mm(v("ph", 0, P), v("G8", rows=8), v("cntb", rows=8), True, True)
     cp(v("N", 0, P), v("ph", 0, P))
 
@@ -264,14 +273,11 @@ def rank_program(g, core, T, topo):
         o = 15 - i
         return v("Bz%d" % (o % 2), o - o % 2, o - o % 2 + 128)
 
-    def row2(s):
-        o = 7 - s
-        return v("Bd%d" % (o % 2), o - o % 2, o - o % 2 + 128)
-
     cLose = col("TA", LOSE // 16)
     Xw = v("X")
+    half = (P - FUSE) // 2
 
-    def top():
+    def pop():
         ts(v("mk"), v("N", 0, P), cA1, Op.is_equal, -1.0, Op.mult)
         scan(v("TM"), v("ST", 0, P), v("mk"), Op.min, Op.mult)
         mm(v("pz", 0, P), v("I"), v("OD"), True, False)
@@ -279,166 +285,167 @@ def rank_program(g, core, T, topo):
         scan(v("SC"), v("RB", 0, P), v("pz", 0, P), Op.add, Op.min)
         ts(v("VU"), v("SC", 15, P, 16), -1.0, Op.mult, 1024.0, Op.add)
         cp(v("KU"), ind(v("nbw"), v("VU")))
+        cp(v("Kh"), v("KU"))
+        mm(v("pn", 0, half), v("Lo"), v("Kh", FUSE, P, 2), True)
+        mm(v("pn", 0, half), v("Up"), v("Kh", FUSE + 1, P, 2))
+        mm(v("pn", half, 2 * half), v("Sh"), v("Kh", FUSE, P, 2))
+        mm(v("pn", half, 2 * half), v("Hi"), v("Kh", FUSE + 1, P, 2), False, True)
+        cp(v("KP"), v("pn", 0, 2 * half))
         mm(v("pz", P, 2 * P), v("Ob"), v("TM"), True, True)
 
-    def windows(r):
-        if r in QA:
-            act(v("Q", P * r, P * r + P), v("pp", 0, P), Fn.Identity, bias=-(35840.0 + 4096.0 * r))
-        else:
-            ts(v("Q", P * r, P * r + P), v("pp", 0, P), -(35840.0 + 4096.0 * r), Op.add)
-        for q in range(4):
-            s = 4 * r + q
-            ts(v("WN", P * s, P * s + P), v("Q", P * r, P * r + P), -2048.0 + 1024.0 * q, Op.max, -1024.0 + 1024.0 * q, Op.min)
-            if s == 6:
-                mm(v("pl", 0, P), v("nkD"), v("C1"))
-            if s < 8:
-                mm(v("pl", 0, P), row2(s), v("WN", P * s, P * s + P), False, s == 7)
-
-    top()
-    if len(PEL) < len(CHUNKS):
-        mm(v("pw", 0, 512), v("I"), v("W", 0, 512), True, True)
-        mm(v("pw", 512, V), v("I"), v("W", 512, V), True, True)
-    cp(v("X", 0, V), v("labi"))
+    pop()
+    for h in (0, 512):
+        ts(v("X", h, h + 512), v("labi", h, h + 512), -1.0 / 1024, Op.mult, -1.0, Op.add)
 
     for t in range(STEPS):
         m = 1 << t
         peer = T.cores[rank ^ m]
-        ne = len(topo.engines(peer, core))
+        got1, got2, got3 = [[("r%d_%d" % (k, t), len(topo.engines(peer, core)))] for k in (1, 2, 3)]
         hi = (rank & m) != 0
+        last = t + 1 == STEPS
         cS0, cE0 = (2, 0) if hi else (0, 2)
         m1s, m1r, m2s, m2r, m3s, m3r = ["m%d%s%d" % (k, x, t) for k in (1, 2, 3) for x in "sr"]
         own0, dat0, yr0, ur0 = (56, 24, 4, 8) if hi else (0, 0, 80, 64)
         gs0, us0, ys0 = (0, 32, 48) if hi else (20, 4, 0)
         nd0 = 64 * t
 
-        for (l0, l1) in CHUNKS:
-            l2 = min(max(l0, XSHARE), l1)
-            if l2 > l0:
-                cp(v("XK", 16 * l0, 16 * l2), ind(Xw, v("KU", l0, l2)))
-            if l1 > l2:
-                act(v("XK", 16 * l2, 16 * l1), ind(Xw, v("KU", l2, l1)))
-        if len(PEL) < len(CHUNKS):
-            tt(v("D"), v("X", 0, V), v("pw"), Op.subtract)
+        act(v("W3", 1, 3 * P, 3), ind(v("W"), v("VU")), scale=-1.0 / 1024)
+        act(v("MS", 61, 48 * P + 30, 48), ind(Xw, v("VU")))
+        scan(v("D"), v("X", 0, V), v("W4"), Op.min, Op.add)
+        for l0 in range(0, FUSE, WCUT):
+            act(v("WK", 16 * l0, 16 * (l0 + WCUT)), ind(v("W"), v("KU", l0, l0 + WCUT)), scale=-1.0 / 1024)
+        cp(v("XK", 0, 16 * XSHARE), ind(Xw, v("KU", 0, XSHARE)))
+        act(v("XK", 16 * XSHARE, 16 * FUSE), ind(Xw, v("KU", XSHARE, FUSE)))
+        for l0 in range(FUSE, P, FCUT):
+            l1 = l0 + FCUT
+            k0, k1 = (l0 - FUSE) // 2, (l1 - FUSE) // 2
+            act(v("XL", 16 * k0, 16 * k1), ind(Xw, v("KP", k0, k1)))
+            tt(v("XM", 16 * k0, 16 * k1), ind(Xw, v("KP", half + k0, half + k1)), v("XL", 16 * k0, 16 * k1), Op.max)
+            scan(v("MS", 48 * l0 + 3, 48 * l1, 6), v("R8", 0, 8 * (l1 - l0)), v("XM", 16 * k0, 16 * k1), Op.add, Op.max)
+        for l0 in range(FUSE, P, WCUT):
+            act(v("DK", 16 * l0, 16 * (l0 + WCUT)), ind(v("D"), v("KU", l0, l0 + WCUT)))
         act(v("C0"), v("N", 0, P), Fn.Relu, bias=cN2)
-        for (l0, l1) in CHUNKS:
-            if l0 in PEL:
-                act(v("WK", 16 * l0, 16 * l1), ind(v("W"), v("KU", l0, l1)))
-            else:
-                act(v("DK", 16 * l0, 16 * l1), ind(v("D"), v("KU", l0, l1)))
-        cp(v("Kf"), v("KU"))
-        cuts = sorted(set([0, XSHARE] + [c[1] for c in CHUNKS]))
-        for l0, l1 in zip(cuts[:-1], cuts[1:]):
-            scan(v("MS", 16 * l0, 16 * l1), v("RB", 0, 16 * (l1 - l0)), v("XK", 16 * l0, 16 * l1), Op.add, Op.min)
-        mm(v("pu", 0, P), v("I"), v("N", 0, P), True)
-        mm(v("pu", 0, P), v("Ob"), v("mk"))
-        mm(v("pp", 0, P), v("kI"), v("N", 0, P), True)
-        mm(v("pp", 0, P), v("kOb"), v("mk"))
-        mm(v("pp", 0, P), v("I32"), v("Kf"))
+        for l0, l1 in ((0, XSHARE), (XSHARE, FUSE)):
+            scan(v("MS", 48 * l0, 48 * l1, 3), v("RN", 0, 16 * (l1 - l0)), v("XK", 16 * l0, 16 * l1), Op.add, Op.max)
         tt(v("E1"), v("SC"), v("pz", P, 2 * P), Op.is_equal)
         scan(v("E2"), v("RZ"), v("E1"), Op.mult, Op.add)
         act(v("vf", 0, 12), v("SC", 15, P, 16), Fn.Identity, bias=1024.0, scale=-1.0)
-        for (l0, l1) in CHUNKS:
-            vu = v("VU", l0 // 16, l1 // 16)
-            tt(v("Zt", l0, l1), ind(v("W"), vu), v("MS", 16 * l0 + 15, 16 * l1, 16), Op.add)
-            tt(v("Z", l0, l1), ind(Xw, vu), v("Zt", l0, l1), Op.min)
-            if l0 not in PEL:
-                cp(v("pz", l0, l1), v("Z", l0, l1))
+        for l0, l1 in CHUNKS:
+            scan(v("Z3", 3 * l0, 3 * l1), v("W3", 3 * l0, 3 * l1), v("MS", 48 * l0 + 45, 48 * l1 + 30, 16), Op.add, Op.max)
+            if l0 >= FUSE:
+                ts(v("pz", l0, l1), v("Z", l0, l1), 4096.0, Op.add)
         ts(v("tp", 0, 12), v("E2", 15, P, 16), 2.0, Op.is_ge, cLose, Op.mult)
         tt(v("tq", 0, 12), v("tp", 0, 12), v("vf", 0, 12), Op.max)
         cp(v("VS", 0, 24, 2), v("tq", 0, 12))
         for c in range(12):
             cp(ind(Xw, v("VS", 2 * c, 2 * c + 1)), v("Z", 16 * c, 16 * c + 16))
-        for (l0, l1) in sorted(CHUNKS, key=lambda c: c[0] not in PEL):
-            if l0 in PEL:
-                for h in (0, 512):
-                    mm(v(PEL[l0], h, h + 512), v("nI"), v("WK", 16 * l0 + h, 16 * l0 + h + 512), True)
-                    mm(v(PEL[l0], h, h + 512), v("I32"), v("XK", 16 * l0 + h, 16 * l0 + h + 512), False, True)
+        for h in (0, 512):
+            mm(v("pa", h, h + 512), v("nI"), v("WK", h, h + 512), True)
+            mm(v("pa", h, h + 512), v("I32"), v("XK", h, h + 512), False, True)
+        for l0, l1 in CHUNKS:
             for i in range(16):
-                if l0 in PEL:
-                    tt(v("CM", P * i + l0, P * i + l1), v(PEL[l0], i, V, 16), v("Z", l0, l1), Op.is_gt)
+                cm = v("CM", 16 * l0 + 64 * i, 16 * l0 + 64 * i + 64)
+                if l0 < FUSE:
+                    tt(cm, v("pa", i, V, 16), v("Z", l0, l1), Op.is_lt)
                 else:
-                    tt(v("CM", P * i + l0, P * i + l1), v("DK", 16 * l0 + i, 16 * l1, 16), v("pz", l0, l1), Op.is_gt)
-                mm(v("ph", l0, l1), row(i), v("CM", P * i + l0, P * i + l1), i == 0, i == 15)
-        for ps, a32, a1, ak in (("pl", "D32", "Dm", "kD"), ("pf", "I32", "I", "kI")):
-            mm(v(ps, 0, P), v(a32), v("ST", 0, P), True)
-            mm(v(ps, 0, P), v(a1), v("TM"))
-            mm(v(ps, 0, P), v(ak), v("mk"))
-            mm(v(ps, 0, P), v(ak), v("C0"))
-        if HA:
-            act(v("hit"), v("ph", 0, P), Fn.Sign)
-        else:
-            ts(v("hit"), v("ph", 0, P), 0.0, Op.is_gt)
+                    tt(cm, v("DK", 16 * l0 + i, 16 * l1, 16), v("pz", l0, l1), Op.is_lt)
+                mm(v("ph", l0, l1), row(i), cm, i == 0, i == 15)
+        mm(v("pu", 0, P), v("I"), v("N", 0, P), True)
+        mm(v("pu", 0, P), v("Ob"), v("mk"))
+        mm(v("pp", 0, P), v("kI"), v("N", 0, P), True)
+        mm(v("pp", 0, P), v("kOb"), v("mk"))
+        mm(v("pp", 0, P), v("I"), v("Kh"))
+        mm(v("pl", 0, P), v("I32"), v("ST", 0, P), True)
+        mm(v("pl", 0, P), v("dB"), v("ones"))
+        mm(v("pl", 0, P), v("I"), v("TM"))
+        mm(v("pl", 0, P), v("kI"), v("mk"))
+        mm(v("pl", 0, P), v("kI"), v("C0"))
+        act(v("hit"), v("ph", 0, P), Fn.Sign)
         mm(v("pp", 0, P), v("LP"), v("hit"), False, True)
         mm(v("pu", 0, P), v("Ob"), v("hit"), False, True)
+        ts(v("fS"), v("pu", 0, P), 9.0, Op.is_ge)
+        scan(v("cS"), v("fS"), v("fS"), Op.add, Op.add)
+        act(v("C1"), v("pu", 0, P), Fn.Relu, bias=cN1, scale=1024.0)
         act(v("U"), v("pu", 0, P))
-        ts(v("fS"), v("U"), 9.0, Op.is_ge)
-        act(v("C1"), v("pu", 0, P), Fn.Relu, bias=cN1)
-        act(v("fE"), v("pu", 0, P), Fn.Relu, bias=1.0, scale=-1.0)
-        scan(v("cS"), v("fS"), v("fS"), Op.add, Op.max)
+        act(v("fE"), v("pu", 0, P), Fn.Relu, bias=1.0, scale=-1.0, acc=col("c4", 0))
         scan(v("cE"), v("fE"), v("fE"), Op.add, Op.max)
         for k in range(2):
-            act(v("junk", P * k, P * k + P), v("cS"), Fn.Sign, bias=col("CC", 12 + k), scale=-1.0, acc=col("LA", cS0 + k))
+            act(v("junk", P * k, P * k + P), v("cS"), Fn.Sign, bias=col("CC", 12 + k), scale=-0.5, acc=col("LA", cS0 + k))
         for r in range(4):
-            windows(r)
-        act(v("LS", 0, P), v("pl", 0, P), Fn.Identity, bias=cBL)
-        mm(v("pf", 0, P), v("nkI"), v("C1"))
+            act(v("Q", P * r, P * r + P), v("pp", 0, P), Fn.Identity, bias=-(35840.0 + 4096.0 * r))
         for s in range(16):
-            mm(v("pf", 0, P), row(s), v("WN", P * s, P * s + P), False, s == 15)
+            r, q = s // 4, s % 4
+            ts(v("WN", P * s, P * s + P), v("Q", P * r, P * r + P), -2048.0 + 1024.0 * q, Op.max, -1024.0 + 1024.0 * q, Op.min)
+            mm(v("pl" if s < 8 else "pf", 0, P), row(s), v("WN", P * s, P * s + P), s == 8, s % 8 == 7)
+        tt(v("LS", 0, P), v("pl", 0, P), v("C1"), Op.subtract)
         ts(v("SU"), v("LA", cS0, cS0 + 2), 0.5, Op.mult, 96.0, Op.add)
-        ts(v(m1s, ys0 + cS0, ys0 + cS0 + 2), v("CC", 14, 16), col("cS", P - 1), Op.subtract, 4096.0, Op.mult)
-        ts(v(m1s, ys0 + cE0, ys0 + cE0 + 2), v("CC", 14, 16), col("cE", P - 1), Op.subtract, 4096.0, Op.mult)
-        act(col("c4", 2), col("cS", P - 1), scale=-4096.0)
-        act(col("c4", 3), col("cE", P - 1), scale=-4096.0)
-        act(v("tS"), v("jf"), Fn.Identity, bias=col("c4", 2), scale=4096.0)
-        act(v("tE"), v("jf"), Fn.Identity, bias=col("c4", 3), scale=4096.0)
-        act(v(m1s, gs0, gs0 + 32), ind(v("LS"), v("SU")), Fn.Identity, bias=-1024.0, scale=cM0)
-        ts(v("t2"), ind(v("LS"), v("SU")), cM1, Op.mult, 1024.0, Op.add)
-        tt(v("NF"), v(m1s, gs0, gs0 + 16), v("t2", 16, 32), Op.add)
-        cp(v("NU"), v("NF"))
-        cp(v("NX"), ind(v("NF"), v("CU")))
-        tt(v(m1s, us0, us0 + 16), v("NF"), v("tS"), Op.max)
-        send(v(m1s), v(m1r, 32, 84) if hi else v(m1r, 4, 56), "r1_%d" % t, peer)
-        act(v(m2s), ind(Xw, v("NU")))
-        send(v(m2s), v(m2r), "r2_%d" % t, peer)
+        ts(v(m1s, ys0 + cS0, ys0 + cS0 + 2), v("CC", 16, 18), col("cS", P - 1), Op.subtract, 2048.0, Op.mult)
+        ts(v(m1s, ys0 + cE0, ys0 + cE0 + 2), v("CC", 14, 16), col("c4", 0), Op.subtract, 4096.0, Op.mult)
+        act(v(m1s, gs0, gs0 + 32), ind(v("LS"), v("SU")), Fn.Identity, bias=cM1k, scale=cM0)
+        cp(v("GH"), ind(v("LS"), v("SU")))
+        mm(v("pn", 0, 16), v("Up"), v("GH", 0, 16), True)
+        mm(v("pn", 0, 16), v("Lo"), v("GH", 16, 32), False, True)
+        ts(v("NU"), v("pn", 0, 16), 1024.0, Op.add)
+        cp(v(m1s, us0, us0 + 16), v("pn", 0, 16))
+        send(v(m1s), v(m1r, 32, 84) if hi else v(m1r, 4, 56), got1[0][0], peer)
+        act(v(m2s, 0, 16 * MSPLIT), ind(Xw, v("NU", 0, MSPLIT)))
+        cp(v(m2s, 16 * MSPLIT, 256), ind(Xw, v("NU", MSPLIT, 16)))
+        send(v(m2s), v(m2r), got2[0][0], peer)
         for k in range(2):
             act(v("junk", P * k, P * k + P), v("cE"), Fn.Sign, bias=col("CC", 12 + k), scale=-1.0, acc=col("LA", cE0 + k))
-        mm(v("ph"), v("I"), v("TRI"), True)
+        scan(v("dl"), v("alt"), v("pn", 0, 16), Op.mult, Op.add)
+        cp(v("NX", 0, 16), v("pn", 0, 16))
+        cp(v("NX", 16, 24), v("pn", 0, 16, 2))
+        cp(v("DR"), ind(v("dl"), v("CU")))
+        mm(v("pd", 0, 384), v("I"), v("TRI"), True)
         for a in range(16):
-            mm(v("ph", a, 512, 16), v("Sel", 128 * a, 128 * a + 128), v("NX", 0, 32))
-            mm(v("ph", a, 512, 16), v("nI"), v("NX", 32, 64), False, a == 15)
-        act(v("AB"), v("ph"), Fn.Abs, scale=4096.0)
-        act(v("ST", 0, P), v("pf", 0, P), Fn.Identity, bias=cBF)
+            mm(v("pd", a, 384, 16), v("Sel", 128 * a, 128 * a + 128), v("NX"))
+        mm(v("pd", 256, 384), v("nI"), v("DR"), False, True)
+        act(v("AB"), v("pd", 0, 384), Fn.Abs, bias=cA, scale=4096.0)
+        tt(v("ST", 0, P), v("pf", 0, P), v("LS", 0, P), Op.add)
         ts(v("N", 0, P), v("U"), 16.0, Op.min)
-        scan(v("AM"), v("RC"), v("AB"), Op.add, Op.min)
-        tt(v(m3s), v("dj"), v("AM", 31, 512, 32), Op.subtract)
-        send(v(m3s), v(m3r), "r3_%d" % t, peer)
+        scan(v("AM"), v("RB"), v("AB"), Op.add, Op.min)
+        ts(v(m3s, 0, 16, 2), v("AM", 15, 256, 32), 16.0, Op.add)
+        tt(v(m3s, 1, 16, 2), v("AM", 31, 256, 32), v("AM", 271, 384, 16), Op.min)
+        send(v(m3s), v(m3r), got3[0][0], peer)
         act(v("GV"), ind(v("ST"), v("SU")))
-        mm(v("pz", 384, 416), v("Sh32"), v("GV"), True, True)
-        act(v(m1r, own0, own0 + 32), v("pz", 384, 416), Fn.Identity, bias=cM1k)
+        mm(v("ps", 0, 32), v("Sh32"), v("GV"), True, True)
+        act(v(m1r, own0, own0 + 32), v("ps", 0, 32), Fn.Identity, bias=cM1k)
         act(v("L4"), v("LA"), Fn.Identity, bias=96.0, scale=0.5)
         tt(v("Lp"), v("L4"), v(m1s, ys0, ys0 + 4), Op.max)
         act(v("ND", nd0 + 16 * cS0, nd0 + 16 * cS0 + 32), ind(v("N"), v("SU")), Fn.Identity, bias=-8.0)
-        for k in range(4):
-            ts(col("O4", k), col(m1r, yr0 + k), col("Lp", k), Op.max, col("TA", 12 + k), Op.min, ext=[("r1_%d" % t, ne)])
+        for k in (cE0, cE0 + 1, cS0, cS0 + 1):
+            ts(col("O4", k), col(m1r, yr0 + k), col("Lp", k), Op.max, col("TA", 12 + k), Op.min, ext=got1)
         cp(ind(v("N"), v("O4")), v("ND", nd0, nd0 + 64))
         cp(ind(v("ST"), v("O4")), v(m1r, dat0, dat0 + 64))
-        if t + 1 < STEPS:
-            top()
-        else:
-            act(v("Zt"), v("ST", 0, P), Fn.Identity, bias=1024.0)
+        if last:
+            act(v("out"), v("ST", 0, P), Fn.Identity, bias=1024.0)
             mm(v("pu", 0, P, rows=8), v("GT"), v("N", 0, P), True, True)
             act(v("SC", rows=8), v("pu", 0, P, rows=8))
-            dma("s", hbm(T.ystk), v("Zt"), "o_stk", DMA + 400)
-            dma("s", hbm(T.ycnt), v("SC", rows=8), "o_cnt", DMA)
-        tt(v("uq"), v(m1r, ur0, ur0 + 16), v("tE"), Op.max, ext=[("r1_%d" % t, ne)])
-        tt(v("up"), v("uq"), v("dj"), Op.min)
-        cp(v("JG"), v("up"))
-        tt(v("MN"), ind(Xw, v("JG")), v(m2r), Op.min, ext=[("r2_%d" % t, ne)])
-        tt(v("oj"), v(m3r), v("up"), Op.max, ext=[("r3_%d" % t, ne)])
+            dma("s", hbm(T.ystk), v("out"), "o_stk", DMA + 2600)
+            dma("s", hbm(T.ycnt), v("SC", rows=8), "o_cnt", DMA + 2200)
+        else:
+            pop()
+        ts(col("c4", 1), col(m1r, yr0 + cE0 + 1), col(m1s, ys0 + cE0 + 1), Op.max, -1.0, Op.mult, ext=got1)
+        act(v("NF"), v(m1r, ur0, ur0 + 16), Fn.Identity, bias=1056.0, ext=got1)
+        act(v("nt"), v("JT"), Fn.Identity, bias=col("c4", 1))
+        tt(v("uq"), v("nt"), v("dj"), Op.max)
+        tt(v("up"), v("uq"), v("NF"), Op.min)
+        ts(v("JG"), v(m1r, ur0, ur0 + 16), 1056.0, Op.add, ext=got1)
+        if last:
+            act(v("XO", 0, V), v("X", 0, V), Fn.Identity, bias=-1024.0, scale=-1024.0)
+            tt(v("OG"), ind(v("XF"), v("JG")), v(m2r), Op.max, ext=got2)
+        else:
+            act(v("OG"), ind(v("XF"), v("JG")))
+        tt(v("oj"), v(m3r), v("up"), Op.min, ext=got3)
         cp(v("JU"), v("oj"))
         for c in range(8):
-            cp(ind(Xw, v("JU", 2 * c, 2 * c + 2)), v("MN", 32 * c, 32 * c + 32))
-    dma("s", hbm(T.ylab), v("X", 0, V), "o_lab", DMA + 2000)
+            ju = v("JU", 2 * c, 2 * c + 2)
+            if last:
+                ts(ind(v("XG"), ju), v("OG", 32 * c, 32 * c + 32), -1024.0, Op.mult, -1024.0, Op.add)
+            else:
+                tt(ind(v("XF"), ju), v("OG", 32 * c, 32 * c + 32), v(m2r, 32 * c, 32 * c + 32), Op.max, ext=got2)
+    dma("s", hbm(T.ylab), v("XO", 0, V), "o_lab", DMA + 2000)
 
     emit(g, T, ops, sender)
     g.wait_ge(T.sem.sent, sent[0])
@@ -449,8 +456,9 @@ def rank_program(g, core, T, topo):
 def choose(ops, deps):
     n = len(ops)
     qs = [o[0] for o in ops]
-    dur = [[float(o[6][m]) for o in ops] for m in range(3)]
-    lat = [[float(o[7][m]) for o in ops] for m in range(3)]
+    nm = len(CYC)
+    dur = [[float(o[6][m]) for o in ops] for m in range(nm)]
+    lat = [[float(o[7][m]) for o in ops] for m in range(nm)]
     covered = [0] * n
     near = []
     for j in range(n):
@@ -469,64 +477,178 @@ def choose(ops, deps):
     for j in range(n):
         for k, hard in near[j]:
             after[k].append((j, hard))
-
-    def tails(order, m):
-        tail = [0.0] * n
-        nxt = {}
-        for j in reversed(order):
-            x = dur[m][j] + lat[m][j]
-            for k, hard in after[j]:
-                x = max(x, dur[m][j] + (lat[m][j] if hard else 0.0) + tail[k])
-            tail[j] = x
-        return tail
+    gaps = [[[(k, lat[m][k] if hard else 0.0) for k, hard in near[j]] for j in range(n)] for m in range(nm)]
+    outs = [[[(k, lat[m][j] if hard else 0.0) for k, hard in after[j]] for j in range(n)] for m in range(nm)]
+    pre = [set(k for k, hard in near[j]) for j in range(n)]
+    suc = [set(k for k, hard in after[j]) for j in range(n)]
+    final = [j for j in range(n) if not after[j]]
 
     def span(order, m):
         free = {}
         end = [0.0] * n
-        last = 0.0
         for j in order:
             t0 = free.get(qs[j], 0.0)
-            for k, hard in near[j]:
-                t0 = max(t0, end[k] + (lat[m][k] if hard else 0.0))
+            for k, x in gaps[m][j]:
+                t0 = max(t0, end[k] + x)
             end[j] = free[qs[j]] = t0 + dur[m][j]
-            last = max(last, end[j] + lat[m][j])
-        return last
+        return max(end[j] + lat[m][j] for j in final)
 
-    def schedule(prio, m):
+    def schedule(m):
+        way = [0.0] * n
+        for j in range(n - 1, -1, -1):
+            way[j] = dur[m][j] + max([lat[m][j]] + [x + way[k] for k, x in outs[m][j]])
         left = [len(d) for d in near]
         ready = [j for j in range(n) if left[j] == 0]
         early = [0.0] * n
-        free = {q: 0.0 for q in "vapgs"}
+        free = {q: 0.0 for q in "vapgsd"}
         order = []
         while ready:
             t0, first = min((max(early[j], free[qs[j]]), j) for j in ready)
             q = qs[first]
-            j = max((prio[k], -k) for k in ready if qs[k] == q and early[k] <= t0 + SLACK)
-            j = -j[1]
-            t0 = max(early[j], free[q])
-            free[q] = t0 + dur[m][j]
+            j = -max((way[k], -k) for k in ready if qs[k] == q and early[k] <= t0 + SLACK)[1]
+            free[q] = max(early[j], free[q]) + dur[m][j]
             ready.remove(j)
             order.append(j)
-            for k, hard in after[j]:
-                early[k] = max(early[k], free[q] + (lat[m][j] if hard else 0.0))
+            for k, x in outs[m][j]:
+                early[k] = max(early[k], free[q] + x)
                 left[k] -= 1
                 if left[k] == 0:
                     ready.append(k)
         return order
 
+    def pack(order, m, back):
+        du = dur[m]
+        start = [0.0] * n
+        busy = {q: ([], []) for q in "vapgsd"}
+        for j in order:
+            t0 = lat[m][j] if back else 0.0
+            for k, x in (outs if back else gaps)[m][j]:
+                t0 = max(t0, start[k] + du[k] + x)
+            a, b = busy[qs[j]]
+            lo, hi = 0, len(b)
+            while lo < hi:
+                mid = (lo + hi) // 2
+                if b[mid] > t0:
+                    hi = mid
+                else:
+                    lo = mid + 1
+            while lo < len(a) and a[lo] < t0 + du[j]:
+                t0 = max(t0, b[lo])
+                lo += 1
+            a.insert(lo, t0)
+            b.insert(lo, t0 + du[j])
+            start[j] = t0
+        return sorted(range(n), key=lambda j: -start[j] - du[j]), sorted(range(n), key=lambda j: start[j])
+
     rng = np.random.default_rng(SEED)
-    base = np.array(tails(range(n), 1))
-    keys = {}
-    kind = np.array([keys.setdefault((o[0], (o[3] + o[2])[0][0].rstrip("012"), len(o[3])), len(keys)) for o in ops])
-    bump = np.zeros(len(keys))
-    best, score = None, None
-    for it in range(TRIES):
-        trial = bump + (rng.normal(0.0, NOISE, len(keys)) * (rng.random(len(keys)) < 0.05) if it else 0.0)
-        order = schedule((base + trial[kind]).tolist(), 1)
-        s = [span(order, m) for m in range(3)]
-        s = s[0] / 0.8 + s[1] + s[2] / 1.3
-        if score is None or s < score:
-            best, score, bump = order, s, trial
+    best = schedule(0)
+    norm = [span(best, m) / WEIGHT[m] for m in range(nm)]
+    score = float(sum(WEIGHT))
+    for m in range(nm):
+        order = schedule(m)
+        for turn in range(TURNS):
+            order = pack(pack(pack(order, m, False)[0], m, True)[0], m, False)[1]
+            s = sum(span(order, x) / norm[x] for x in range(nm))
+            if s < score:
+                best, score = order, s
+
+    order = best[:]
+    banned = {}
+    since = 0
+    for it in range(MOVES):
+        place = [0] * n
+        line = {q: [] for q in "vapgsd"}
+        at = [0] * n
+        for i, j in enumerate(order):
+            place[j] = i
+            at[j] = len(line[qs[j]])
+            line[qs[j]].append(j)
+        before, behind = [n] * n, [n] * n
+        for l in line.values():
+            for a, b in zip(l[:-1], l[1:]):
+                before[b], behind[a] = a, b
+        ready, end, rest, tail, whole = [], [], [], [], []
+        for m in range(nm):
+            du, ga, ou, la = dur[m], gaps[m], outs[m], lat[m]
+            r, e, s, t = [0.0] * n, [0.0] * (n + 1), [0.0] * n, [0.0] * (n + 1)
+            for j in order:
+                t0 = 0.0
+                for k, x in ga[j]:
+                    if e[k] + x > t0:
+                        t0 = e[k] + x
+                r[j] = t0
+                e[j] = (t0 if t0 > e[before[j]] else e[before[j]]) + du[j]
+            for j in reversed(order):
+                t0 = la[j]
+                for k, x in ou[j]:
+                    if t[k] + x > t0:
+                        t0 = t[k] + x
+                s[j] = t0
+                t[j] = (t0 if t0 > t[behind[j]] else t[behind[j]]) + du[j]
+            ready.append(r)
+            end.append(e)
+            rest.append(s)
+            tail.append(t)
+            whole.append(max(e[j] + la[j] for j in final))
+        now = sum(whole[m] / norm[m] for m in range(nm))
+        if now < score - 1e-9:
+            best, score, since = order[:], now, it
+        elif it - since > PATIENCE:
+            order, since, banned = best[:], it, {}
+            continue
+        m0 = it % nm
+        e, t = end[m0], tail[m0]
+        pairs = [(before[j], j) for j in range(n) if before[j] < n and e[before[j]] + t[j] > whole[m0] - 0.5
+                 and ready[m0][j] < e[before[j]] - 0.5]
+        tried = []
+        for x in rng.permutation(len(pairs))[:WIDTH].tolist():
+            a, b = pairs[x]
+            l = line[qs[a]]
+            far = int(rng.geometric(0.3)) - 1
+            for early in (True, False):
+                i0, i1 = (max(at[a] - far, 0), at[b]) if early else (at[a], min(at[b] + far, len(l) - 1))
+                seg = l[i0:i1 + 1]
+                one = seg[-1] if early else seg[0]
+                if banned.get(one, -1) > it:
+                    continue
+                seg = [one] + seg[:-1] if early else seg[1:] + [one]
+                guess = 0.0
+                for m in range(nm):
+                    du, r, s = dur[m], ready[m], rest[m]
+                    t0 = end[m][before[l[i0]]]
+                    heads = []
+                    for j in seg:
+                        t0 = t0 if t0 > r[j] else r[j]
+                        heads.append(t0)
+                        t0 += du[j]
+                    t0 = tail[m][behind[l[i1]]]
+                    worst, was = 0.0, 0.0
+                    for j, h in zip(seg[::-1], heads[::-1]):
+                        t0 = (t0 if t0 > s[j] else s[j]) + du[j]
+                        worst = max(worst, h + t0)
+                        was = max(was, end[m][j] - du[j] + tail[m][j])
+                    guess += (worst if was > whole[m] - 0.5 else max(worst, whole[m])) / norm[m]
+                tried.append((guess, i0, i1, early, qs[a]))
+        tried.sort()
+        for guess, i0, i1, early, q in tried:
+            a, b = line[q][i0], line[q][i1]
+            part = order[place[a]:place[b] + 1]
+            one, other, links, beside = (b, a, pre, before) if early else (a, b, suc, behind)
+            took, want = [one], set(links[one])
+            for k in (part[-2::-1] if early else part[1:]):
+                if k in want:
+                    if qs[k] == q:
+                        break
+                    took.append(k)
+                    want |= links[k]
+                    want.add(beside[k])
+            else:
+                moved = set(took)
+                stay = [k for k in part if k not in moved]
+                order[place[a]:place[b] + 1] = took[::-1] + stay if early else stay + took
+                banned[one] = it + 5 + int(rng.integers(0, 10))
+                banned[other] = it + 3
+                break
     return best
 
 
@@ -537,30 +659,35 @@ def emit(g, T, ops, sender):
     for j, (q, call, rd, wr, sem, ext, dur, lat) in enumerate(ops):
         d = {}
         for acc, w in [(x, False) for x in rd] + [(x, True) for x in wr]:
-            name, a, b = acc
+            name, a, b, st = acc
             ps = SCRATCH[name][0] == "psum"
             lo, hi = (a // 512 * 512, (b + 511) // 512 * 512) if ps else (a, b)
-            for (k, l2, h2, w2, a2, b2) in log.get(name, []):
+            for (k, l2, h2, w2, a2, b2, st2) in log.get(name, []):
                 if l2 >= hi or lo >= h2 or k == j:
+                    continue
+                if not ps and st * st2 > 1 and not set(range(a, b, st)) & set(range(a2, b2, st2)):
                     continue
                 if ops[k][0] != q or ops[k][4] is not None or sem is not None:
                     if w or w2 or ps:
                         d[k] = True
                 elif q == "p":
-                    d[k] = False
+                    if ps:
+                        d[k] = False
                 elif a2 < b and a < b2 and (w or w2):
                     d[k] = True
-            log.setdefault(name, []).append((j, lo, hi, w, a, b))
+            log.setdefault(name, []).append((j, lo, hi, w, a, b, st))
         for s, c in ext:
             d[sender[s]] = True
-        if j in (2, 3, 4):
+        if q == "d":
+            d[j - 1] = True
+        if j in (2, 3, 4, 5):
             d[0 if j == 2 else j - 1] = None
         deps.append(d)
     if not ORDER:
         ORDER.extend(choose(ops, deps))
-    order = ORDER
-    place = {j: i for i, j in enumerate(order)}
-    assert len(order) == n and all(place[k] < place[j] for j in range(n) for k in deps[j])
+    order = [j for j in ORDER if ops[j][0] != "d"]
+    place = {j: i for i, j in enumerate(ORDER)}
+    assert len(ORDER) == n and all(place[k] < place[j] for j in range(n) for k in deps[j])
     queues = {"v": g.vector, "a": g.scalar, "p": g.tensor, "g": g, "s": g.sync}
     counter = {"v": "cv", "a": "ca", "p": "cp", "g": "cg"}
     seen = {}

import numpy as np
from concourse.mybir import AluOpType as Op, ActivationFunctionType as Fn

V, P, STEPS = 1024, 192, 3
BIG = float(2 ** 21)
LOSE = 1040
CHUNKS = ((0, 64), (64, 128), (128, 192))
FUSE = 64
XSHARE = 16
WCUT, FCUT = 32, 64
MSPLIT = 8
LOADS = ("nb", "ln", "lab")
ALIAS = {"pd": ("pa", 512, 512), "ps": ("pa", 0, 512), "pn": ("ph", 0, 512)}
CYC = np.array([0.83, 1.1, 1.0, 0.95, 1.15])
GATH = np.array([1.56, 1.5, 1.2, 2.05, 1.8])
SCAT = np.array([3.8, 3.8, 5.0, 4.5, 2.2])
PEC = CYC * np.array([0.5, 0.5, 0.85, 0.5, 0.85])
HOP = np.array([180.0, 130.0, 230.0, 150.0, 180.0])
FAR = np.array([900.0, 600.0, 1200.0, 1000.0, 1800.0]) + HOP
LINK = np.array([216.0, 280.0, 200.0, 200.0, 120.0])
ISSUE = np.array([450.0, 450.0, 300.0, 450.0, 700.0])
ROWS = np.array([290.0, 160.0, 500.0, 300.0, 300.0])
WEIGHT = (1.5, 1.5, 0.5, 1.5, 0.5)
ACT, DMA, LOAD, SLACK = 90.0, 2000.0, 800.0, 60.0
TURNS, MOVES, WIDTH, PATIENCE, SEED = 6, 2000, 40, 100, 0
ORDER = []
f32, bf, f16, i32, u16 = "float32", "bfloat16", "float16", "int32", "uint16"


def _scratch():
    s = {}

    def sb(dt, **k):
        for n, w in k.items():
            s[n] = ("sbuf", [128, w], dt)
    sb(i32, nbw=1032, labi=1024, stki=192, cnti=192, pi=2)
    sb(f32, XF=1104, XG=1064, D=1024, W4=1024, XK=1024, XL=1024, XM=1024, DK=3072, MS=9248, W3=576, Z3=576, OG=256, ST=256,
       LS=200, SC=192, out=192, CC=32, TA=80, k16=80, jr=16, JT=16, vf=16, tp=16, tq=16, up=16, uq=16, LA=4, L4=4, Lp=4, NF=16,
       nt=16, oj=16, dj=16, dl=16, I32=128, Sh32=128, GV=32, c4=2)
    sb(bf, W=1040, WK=1024, CM=3072, N=256, U=192, mk=192, C0=192, C1=192, hit=192, fS=192, fE=192, cS=192, cE=192, junk=384,
       E1=192, E2=192, AB=384, AM=384, RB=384, RN=1024, R8=512, RZ=192, ones=192, kk=128, ar=256, xr=160, OD=192, TRI=384,
       alt=16, cntb=192, ND=64 * STEPS, G8=128, GT=8, Ob=128, I=128, nI=128, kI=128, kOb=128, dB=128, LP=128, Up=128, Lo=128,
       Hi=128, Sh=128, Bz0=160, Bz1=160, Sel=2048)
    sb(f16, TM=192, Kh=192, GH=32, Q=4 * 192, WN=16 * 192, NX=24, DR=128)
    sb(u16, VU=12, VS=24, KU=192, KP=128, SU=2, NU=16, CU=8, O4=4, JU=16, JG=16)
    ALIAS["X"], ALIAS["XO"] = ("XF", 32, 1072), ("XG", 32, 1024)
    for n, w in (("m1s", 52), ("m1r", 88), ("m2s", 256), ("m2r", 256), ("m3s", 16), ("m3r", 16)):
        sb(f32, **{n: w * STEPS})
        for t in range(STEPS):
            ALIAS["%s%d" % (n, t)] = (n, w * t, w)
    for n in ("pz", "ph", "pp", "pu", "pl", "pf"):
        s[n] = ("psum", [128, 512], f32)
    s["pa"] = ("psum", [128, 1024], f32)
    return s


SCRATCH = _scratch()
SEMAPHORES = (["cv", "ca", "cp", "cg", "sent", "l_stk", "l_cnt", "l_nb", "l_lab0", "l_lab1", "l_ln", "o_lab", "o_stk", "o_cnt"]
              + ["r%d_%d" % (k, t) for k in (1, 2, 3) for t in range(STEPS)])


def rank_program(g, core, T, topo):
    rank = T.rank_of(core)
    if rank is None:
        return
    ops = []

    def v(name, lo=0, hi=None, step=1, rows=128):
        if name == "Z":
            name, lo, hi, step = "Z3", 3 * lo + 1, 3 * hi, 3
        if name in ALIAS:
            name, at, w = ALIAS[name]
            lo, hi = at + lo, at + (w if hi is None else hi)
        t = T[name]
        hi = t.shape[1] if hi is None else hi
        ap = t[0:rows, lo:hi] if step == 1 else t[0:rows, lo:hi:step]
        return (ap, [(name, lo, hi, step)], len(range(lo, hi, step)), SCRATCH[name][2] in (bf, f16, u16), SCRATCH[name][0] == "psum", False)

    def col(name, k):
        return v(name, k, k + 1)

    def ind(win, off):
        return (win[0].indirect(off[0]), win[1] + off[1], 16 * off[2], False, False, True)

    def sc(x):
        return x[0] if isinstance(x, tuple) else x

    def cost(q, o, ins, two):
        if q == "p":
            return max(64, ins[1][2]) * PEC * (1 if ins[0][3] else 4)
        if q == "g":
            return 170 + 2 * o[2] * CYC
        full = [x for x in ins if isinstance(x, tuple)][:2 if two else 1]
        if o[5]:
            return 50 + o[2] * SCAT * CYC
        if full and full[0][5]:
            return 60 + o[2] * GATH * CYC
        k = 1.0
        if two == 1:
            k = 1.0 if any(x[4] for x in full) else 2.0
        elif q == "v" and o[3] and all(x[3] for x in full):
            k = 0.5
        return max(64, o[2] * k) * CYC + (ACT if q == "a" else 0)

    def add(q, call, out, ins, sem=None, ext=(), two=0, dur=None, lat=HOP):
        wr = []
        rd = []
        for o in out:
            wr += o[1][:1]
            rd += o[1][1:]
        for x in ins:
            if isinstance(x, tuple):
                rd += x[1]
        if dur is None:
            dur = cost(q, out[0], ins, two)
        ops.append((q, call, rd, wr, sem, list(ext), dur + 0 * CYC, lat + 0 * CYC))

    def cp(o, a, ext=()):
        add("v", lambda: g.vector.tensor_copy(o[0], a[0]), [o], [a], ext=ext)

    def tt(o, a, b, op, ext=()):
        add("v", lambda: g.vector.tensor_tensor(o[0], a[0], b[0], op), [o], [a, b], ext=ext, two=1)

    def ts(o, a, s1, op0, s2=None, op1=None, ext=()):
        if op1 is None:
            add("v", lambda: g.vector.tensor_scalar(o[0], a[0], sc(s1), None, op0), [o], [a, s1], ext=ext)
        else:
            add("v", lambda: g.vector.tensor_scalar(o[0], a[0], sc(s1), sc(s2), op0, op1), [o], [a, s1, s2], ext=ext)

    def scan(o, a, b, op0, op1, ext=()):
        add("v", lambda: g.vector.tensor_tensor_scan(o[0], a[0], b[0], 0.0, op0, op1), [o], [a, b], ext=ext, two=2)

    def ms(o, c):
        add("v", lambda: g.vector.memset(o[0], c), [o], [])

    def act(o, a, fn=Fn.Copy, bias=None, scale=None, acc=None, ext=()):
        kw = {}
        if bias is not None:
            kw["bias"] = sc(bias)
        if scale is not None:
            kw["scale"] = sc(scale)
        if acc is not None:
            kw["accum_out"] = acc[0]
        add("a", lambda: g.scalar.activation(o[0], a[0], fn, **kw), [o] + ([acc] if acc else []), [a, bias, scale], ext=ext)

    def mm(o, l, r, start=False, stop=False):
        add("p", lambda: g.tensor.matmul(o[0], l[0], r[0], start, stop), [o], [l, r])

    def iota(o, pat, base=0, cm=0):
        if o[1][0][0] == "pi":
            add("g", lambda: g.iota(o[0], pat, base, cm), [o], [])
        else:
            add("g", lambda: g.iota(o[0], pat, base, cm, allow_small_or_imprecise_dtypes=True), [o], [])

    def sel(o, a, pat, op, base, cm, fill=0.0):
        add("g", lambda: g.affine_select(o[0], a[0], pat, op, fill, base, cm), [o], [a])

    def dma(q, o, a, sem, lat):
        e = g.sync if q == "s" else g.scalar
        add(q, lambda: e.dma_start(o[0], a[0]), [o], [a], sem=sem, dur=60.0, lat=lat)

    sent = [0]
    sender = {}

    def send(src, dst, sem, peer):
        rid, pid = topo.addr(peer, core)
        mask = topo.mask(core, peer)
        sent[0] += len(topo.engines(core, peer))
        add("g", lambda: g.remote_dma(dst[0], src[0], T.sem[sem], T.sem.sent, pid, rid, mask), [], [src], sem="sent",
            dur=ISSUE, lat=0.0)
        add("d", None, [], [], sem="sent", dur=ROWS + 512 * src[2] / LINK, lat=FAR)
        sender[sem] = len(ops) - 1

    def hbm(t):
        return (t[:], [])

    dma("s", v("stki"), hbm(T.stk), "l_stk", DMA)
    dma("a", v("cnti", rows=8), hbm(T.cnt), "l_cnt", DMA - 400)
    late = DMA
    for name in LOADS:
        if name == "lab":
            for h in (0, 1):
                late += LOAD
                dma("s", v("labi", 512 * h, 512 * h + 512), (T.lab[:, 512 * h:512 * h + 512], []), "l_lab%d" % h, late)
        elif name == "nb":
            late += 2 * LOAD
            dma("s", v("nbw", 0, V), hbm(T.nb), "l_nb", late)
        else:
            late += LOAD
            dma("s", v("W", 0, V), hbm(T.ln), "l_ln", late)

    one = v("ones", 0, 128)
    ms(v("ones"), 1.0)
    iota(col("pi", 0), [[0, 1]], 0, 1)
    iota(v("ar"), [[0, 16], [1, 16]])
    sel(v("G8"), one, [[1, 8], [0, 16]], Op.is_equal, 0, -1)
    sel(v("Ob"), one, [[-16, 8], [0, 16]], Op.is_ge, 0, 1)
    sel(v("Ob"), v("Ob"), [[16, 8], [0, 16]], Op.is_ge, 15, -1)
    sel(v("I"), one, [[-1, 128]], Op.is_equal, 0, 1)
    iota(v("k16"), [[16, 80]])
    iota(v("xr"), [[1, 160]])
    ms(v("kk"), 1024.0)
    for name, w, gap, fill, mark in (("RB", 384, 16, 0.0, 2 * BIG), ("RN", V, 16, 0.0, -4096.0), ("RZ", P, 16, 1.0, 0.0),
                                     ("R8", 512, 8, 0.0, -4096.0), ("alt", 16, 2, -1.0, 0.0)):
        ms(v(name), fill)
        ms(v(name, 0, w, gap), mark)
    ms(v("ST", P), 0.0)
    ms(v("N", P), 0.0)
    ms(v("LS", P), -1024.0)
    ms(v("ND"), 8.0)
    ms(v("X", V), -2048.0)
    ms(v("XF", 0, 32), -2048.0)
    ms(v("MS", 77, 48 * P + 30, 48), -4096.0)
    ms(v("W3", 0, 3 * P, 3), -4096.0)
    ms(v("W3", 2, 3 * P, 3), 0.0)
    ms(v("W", V), BIG)
    ms(v("nbw", V), 0)
    ms(v("TRI", 256, 384), 0.0)
    a_i = col("pi", 1)
    ts(a_i, col("pi", 0), 15, Op.bitwise_and)
    cA, cA1, cN1, cN2, cM0, cBF, cM1k, cG15, cG14, cJ, cG, cH = [col("CC", k) for k in range(12)]
    cp(cA, a_i)
    ts(cA1, a_i, 1.0, Op.add)
    ts(cN1, a_i, -1024.0, Op.mult, -1024.0, Op.add)
    ts(cN2, a_i, -1.0, Op.mult, -2.0, Op.add)
    ts(cM0, a_i, 8.0, Op.is_lt)
    ts(cM1k, a_i, 8.0, Op.is_ge, -1024.0, Op.mult)
    ts(cH, a_i, 8.0, Op.is_lt, -0.5, Op.add)
    tt(cG, col("pi", 0), a_i, Op.subtract)
    ts(v("OD"), v("ar", 0, P), cA, Op.not_equal, 4096.0, Op.mult)
    ts(col("pi", 0), a_i, 3, Op.bitwise_and)
    ts(cG15, cG, 15.0, Op.add)
    ts(cG14, cG, 14.0, Op.add)
    ts(cJ, cA, 2.0, Op.mult, cH, Op.add)
    ts(cBF, col("pi", 0), -16384.0, Op.mult, 32768.0, Op.add)
    ts(v("dB"), v("I"), cBF, Op.mult)
    for name, base in (("Up", 128), ("Lo", 0), ("Sh", -8), ("Hi", 120)):
        sel(v(name), one, [[-16, 8], [-128, 2], [-1, 8]], Op.is_equal, base, 1)
    sel(v("LP"), v("kk"), [[-16, 8], [0, 16]], Op.is_ge, 0, 1)
    sel(v("LP"), v("LP"), [[1, 128]], Op.is_ge, 0, -1)
    sel(v("LP"), v("LP"), [[1, 128]], Op.not_equal, 0, -1, 33792.0)
    iota(v("jr"), [[-2, 16]])
    iota(v("dj"), [[0, 8], [-16, 2]], 16)
    act(v("nI"), v("I"), scale=-1.0)
    for a in range(16):
        sel(v("Sel", 128 * a, 128 * a + 128), v("nI"), [[16, 8], [0, 16]], Op.not_equal, a, -1, 1.0)
        sel(v("Sel", 129 * a, 128 * a + 128, 16), v("Sel", 129 * a, 128 * a + 128, 16), [[16, 8]], Op.not_equal, a, -1)
    sel(v("GT"), v("ones", 0, 8), [[16, 8]], Op.is_equal, 0, -1)
    act(v("I32"), v("I"))
    act(v("kI"), v("I"), scale=1024.0)
    act(v("kOb"), v("Ob"), scale=1024.0)
    act(v("Sh32"), v("Sh"))
    for h in (0, 512):
        act(v("W4", h, h + 512), v("W", h, h + 512), Fn.Identity, bias=4096.0, scale=1.0 / 1024)
    ts(v("TA"), v("k16"), cA, Op.add)
    ts(v("Bz0"), v("xr"), cG15, Op.is_equal)
    ts(v("Bz1"), v("xr"), cG14, Op.is_equal)
    for k in range(2):
        ts(col("CC", 12 + k), a_i, 2.0, Op.mult, 1.5 - k, Op.add)
        ts(col("CC", 14 + k), a_i, 2.0, Op.mult, 2.0 - k, Op.add)
        ts(col("CC", 16 + k), a_i, 4.0, Op.mult, 4.0 - 2 * k, Op.add)
    ts(v("JT"), v("jr"), cJ, Op.add, 4096.0, Op.mult)
    ts(v("dj"), v("dj"), cA, Op.add)
    ts(v("TRI", 0, 256), v("ar"), cA, Op.is_ge, 4096.0, Op.mult)
    cp(v("CU"), v("xr", 1, 16, 2))

    cp(v("cntb", rows=8), v("cnti", rows=8))
    ts(v("ST", 0, P), v("stki"), -1024.0, Op.add)
    mm(v("ph", 0, P), v("G8", rows=8), v("cntb", rows=8), True, True)
    cp(v("N", 0, P), v("ph", 0, P))

    def row(i):
        o = 15 - i
        return v("Bz%d" % (o % 2), o - o % 2, o - o % 2 + 128)

    cLose = col("TA", LOSE // 16)
    Xw = v("X")
    half = (P - FUSE) // 2

    def pop():
        ts(v("mk"), v("N", 0, P), cA1, Op.is_equal, -1.0, Op.mult)
        scan(v("TM"), v("ST", 0, P), v("mk"), Op.min, Op.mult)
        mm(v("pz", 0, P), v("I"), v("OD"), True, False)
        mm(v("pz", 0, P), v("Ob"), v("TM"), False, True)
        scan(v("SC"), v("RB", 0, P), v("pz", 0, P), Op.add, Op.min)
        ts(v("VU"), v("SC", 15, P, 16), -1.0, Op.mult, 1024.0, Op.add)
        cp(v("KU"), ind(v("nbw"), v("VU")))
        cp(v("Kh"), v("KU"))
        mm(v("pn", 0, half), v("Lo"), v("Kh", FUSE, P, 2), True)
        mm(v("pn", 0, half), v("Up"), v("Kh", FUSE + 1, P, 2))
        mm(v("pn", half, 2 * half), v("Sh"), v("Kh", FUSE, P, 2))
        mm(v("pn", half, 2 * half), v("Hi"), v("Kh", FUSE + 1, P, 2), False, True)
        cp(v("KP"), v("pn", 0, 2 * half))
        mm(v("pz", P, 2 * P), v("Ob"), v("TM"), True, True)

    pop()
    for h in (0, 512):
        ts(v("X", h, h + 512), v("labi", h, h + 512), -1.0 / 1024, Op.mult, -1.0, Op.add)

    for t in range(STEPS):
        m = 1 << t
        peer = T.cores[rank ^ m]
        got1, got2, got3 = [[("r%d_%d" % (k, t), len(topo.engines(peer, core)))] for k in (1, 2, 3)]
        hi = (rank & m) != 0
        last = t + 1 == STEPS
        cS0, cE0 = (2, 0) if hi else (0, 2)
        m1s, m1r, m2s, m2r, m3s, m3r = ["m%d%s%d" % (k, x, t) for k in (1, 2, 3) for x in "sr"]
        own0, dat0, yr0, ur0 = (56, 24, 4, 8) if hi else (0, 0, 80, 64)
        gs0, us0, ys0 = (0, 32, 48) if hi else (20, 4, 0)
        nd0 = 64 * t

        act(v("W3", 1, 3 * P, 3), ind(v("W"), v("VU")), scale=-1.0 / 1024)
        act(v("MS", 61, 48 * P + 30, 48), ind(Xw, v("VU")))
        scan(v("D"), v("X", 0, V), v("W4"), Op.min, Op.add)
        for l0 in range(0, FUSE, WCUT):
            act(v("WK", 16 * l0, 16 * (l0 + WCUT)), ind(v("W"), v("KU", l0, l0 + WCUT)), scale=-1.0 / 1024)
        cp(v("XK", 0, 16 * XSHARE), ind(Xw, v("KU", 0, XSHARE)))
        act(v("XK", 16 * XSHARE, 16 * FUSE), ind(Xw, v("KU", XSHARE, FUSE)))
        for l0 in range(FUSE, P, FCUT):
            l1 = l0 + FCUT
            k0, k1 = (l0 - FUSE) // 2, (l1 - FUSE) // 2
            act(v("XL", 16 * k0, 16 * k1), ind(Xw, v("KP", k0, k1)))
            tt(v("XM", 16 * k0, 16 * k1), ind(Xw, v("KP", half + k0, half + k1)), v("XL", 16 * k0, 16 * k1), Op.max)
            scan(v("MS", 48 * l0 + 3, 48 * l1, 6), v("R8", 0, 8 * (l1 - l0)), v("XM", 16 * k0, 16 * k1), Op.add, Op.max)
        for l0 in range(FUSE, P, WCUT):
            act(v("DK", 16 * l0, 16 * (l0 + WCUT)), ind(v("D"), v("KU", l0, l0 + WCUT)))
        act(v("C0"), v("N", 0, P), Fn.Relu, bias=cN2)
        for l0, l1 in ((0, XSHARE), (XSHARE, FUSE)):
            scan(v("MS", 48 * l0, 48 * l1, 3), v("RN", 0, 16 * (l1 - l0)), v("XK", 16 * l0, 16 * l1), Op.add, Op.max)
        tt(v("E1"), v("SC"), v("pz", P, 2 * P), Op.is_equal)
        scan(v("E2"), v("RZ"), v("E1"), Op.mult, Op.add)
        act(v("vf", 0, 12), v("SC", 15, P, 16), Fn.Identity, bias=1024.0, scale=-1.0)
        for l0, l1 in CHUNKS:
            scan(v("Z3", 3 * l0, 3 * l1), v("W3", 3 * l0, 3 * l1), v("MS", 48 * l0 + 45, 48 * l1 + 30, 16), Op.add, Op.max)
            if l0 >= FUSE:
                ts(v("pz", l0, l1), v("Z", l0, l1), 4096.0, Op.add)
        ts(v("tp", 0, 12), v("E2", 15, P, 16), 2.0, Op.is_ge, cLose, Op.mult)
        tt(v("tq", 0, 12), v("tp", 0, 12), v("vf", 0, 12), Op.max)
        cp(v("VS", 0, 24, 2), v("tq", 0, 12))
        for c in range(12):
            cp(ind(Xw, v("VS", 2 * c, 2 * c + 1)), v("Z", 16 * c, 16 * c + 16))
        for h in (0, 512):
            mm(v("pa", h, h + 512), v("nI"), v("WK", h, h + 512), True)
            mm(v("pa", h, h + 512), v("I32"), v("XK", h, h + 512), False, True)
        for l0, l1 in CHUNKS:
            for i in range(16):
                cm = v("CM", 16 * l0 + 64 * i, 16 * l0 + 64 * i + 64)
                if l0 < FUSE:
                    tt(cm, v("pa", i, V, 16), v("Z", l0, l1), Op.is_lt)
                else:
                    tt(cm, v("DK", 16 * l0 + i, 16 * l1, 16), v("pz", l0, l1), Op.is_lt)
                mm(v("ph", l0, l1), row(i), cm, i == 0, i == 15)
        mm(v("pu", 0, P), v("I"), v("N", 0, P), True)
        mm(v("pu", 0, P), v("Ob"), v("mk"))
        mm(v("pp", 0, P), v("kI"), v("N", 0, P), True)
        mm(v("pp", 0, P), v("kOb"), v("mk"))
        mm(v("pp", 0, P), v("I"), v("Kh"))
        mm(v("pl", 0, P), v("I32"), v("ST", 0, P), True)
        mm(v("pl", 0, P), v("dB"), v("ones"))
        mm(v("pl", 0, P), v("I"), v("TM"))
        mm(v("pl", 0, P), v("kI"), v("mk"))
        mm(v("pl", 0, P), v("kI"), v("C0"))
        act(v("hit"), v("ph", 0, P), Fn.Sign)
        mm(v("pp", 0, P), v("LP"), v("hit"), False, True)
        mm(v("pu", 0, P), v("Ob"), v("hit"), False, True)
        ts(v("fS"), v("pu", 0, P), 9.0, Op.is_ge)
        scan(v("cS"), v("fS"), v("fS"), Op.add, Op.add)
        act(v("C1"), v("pu", 0, P), Fn.Relu, bias=cN1, scale=1024.0)
        act(v("U"), v("pu", 0, P))
        act(v("fE"), v("pu", 0, P), Fn.Relu, bias=1.0, scale=-1.0, acc=col("c4", 0))
        scan(v("cE"), v("fE"), v("fE"), Op.add, Op.max)
        for k in range(2):
            act(v("junk", P * k, P * k + P), v("cS"), Fn.Sign, bias=col("CC", 12 + k), scale=-0.5, acc=col("LA", cS0 + k))
        for r in range(4):
            act(v("Q", P * r, P * r + P), v("pp", 0, P), Fn.Identity, bias=-(35840.0 + 4096.0 * r))
        for s in range(16):
            r, q = s // 4, s % 4
            ts(v("WN", P * s, P * s + P), v("Q", P * r, P * r + P), -2048.0 + 1024.0 * q, Op.max, -1024.0 + 1024.0 * q, Op.min)
            mm(v("pl" if s < 8 else "pf", 0, P), row(s), v("WN", P * s, P * s + P), s == 8, s % 8 == 7)
        tt(v("LS", 0, P), v("pl", 0, P), v("C1"), Op.subtract)
        ts(v("SU"), v("LA", cS0, cS0 + 2), 0.5, Op.mult, 96.0, Op.add)
        ts(v(m1s, ys0 + cS0, ys0 + cS0 + 2), v("CC", 16, 18), col("cS", P - 1), Op.subtract, 2048.0, Op.mult)
        ts(v(m1s, ys0 + cE0, ys0 + cE0 + 2), v("CC", 14, 16), col("c4", 0), Op.subtract, 4096.0, Op.mult)
        act(v(m1s, gs0, gs0 + 32), ind(v("LS"), v("SU")), Fn.Identity, bias=cM1k, scale=cM0)
        cp(v("GH"), ind(v("LS"), v("SU")))
        mm(v("pn", 0, 16), v("Up"), v("GH", 0, 16), True)
        mm(v("pn", 0, 16), v("Lo"), v("GH", 16, 32), False, True)
        ts(v("NU"), v("pn", 0, 16), 1024.0, Op.add)
        cp(v(m1s, us0, us0 + 16), v("pn", 0, 16))
        send(v(m1s), v(m1r, 32, 84) if hi else v(m1r, 4, 56), got1[0][0], peer)
        act(v(m2s, 0, 16 * MSPLIT), ind(Xw, v("NU", 0, MSPLIT)))
        cp(v(m2s, 16 * MSPLIT, 256), ind(Xw, v("NU", MSPLIT, 16)))
        send(v(m2s), v(m2r), got2[0][0], peer)
        for k in range(2):
            act(v("junk", P * k, P * k + P), v("cE"), Fn.Sign, bias=col("CC", 12 + k), scale=-1.0, acc=col("LA", cE0 + k))
        scan(v("dl"), v("alt"), v("pn", 0, 16), Op.mult, Op.add)
        cp(v("NX", 0, 16), v("pn", 0, 16))
        cp(v("NX", 16, 24), v("pn", 0, 16, 2))
        cp(v("DR"), ind(v("dl"), v("CU")))
        mm(v("pd", 0, 384), v("I"), v("TRI"), True)
        for a in range(16):
            mm(v("pd", a, 384, 16), v("Sel", 128 * a, 128 * a + 128), v("NX"))
        mm(v("pd", 256, 384), v("nI"), v("DR"), False, True)
        act(v("AB"), v("pd", 0, 384), Fn.Abs, bias=cA, scale=4096.0)
        tt(v("ST", 0, P), v("pf", 0, P), v("LS", 0, P), Op.add)
        ts(v("N", 0, P), v("U"), 16.0, Op.min)
        scan(v("AM"), v("RB"), v("AB"), Op.add, Op.min)
        ts(v(m3s, 0, 16, 2), v("AM", 15, 256, 32), 16.0, Op.add)
        tt(v(m3s, 1, 16, 2), v("AM", 31, 256, 32), v("AM", 271, 384, 16), Op.min)
        send(v(m3s), v(m3r), got3[0][0], peer)
        act(v("GV"), ind(v("ST"), v("SU")))
        mm(v("ps", 0, 32), v("Sh32"), v("GV"), True, True)
        act(v(m1r, own0, own0 + 32), v("ps", 0, 32), Fn.Identity, bias=cM1k)
        act(v("L4"), v("LA"), Fn.Identity, bias=96.0, scale=0.5)
        tt(v("Lp"), v("L4"), v(m1s, ys0, ys0 + 4), Op.max)
        act(v("ND", nd0 + 16 * cS0, nd0 + 16 * cS0 + 32), ind(v("N"), v("SU")), Fn.Identity, bias=-8.0)
        for k in (cE0, cE0 + 1, cS0, cS0 + 1):
            ts(col("O4", k), col(m1r, yr0 + k), col("Lp", k), Op.max, col("TA", 12 + k), Op.min, ext=got1)
        cp(ind(v("N"), v("O4")), v("ND", nd0, nd0 + 64))
        cp(ind(v("ST"), v("O4")), v(m1r, dat0, dat0 + 64))
        if last:
            act(v("out"), v("ST", 0, P), Fn.Identity, bias=1024.0)
            mm(v("pu", 0, P, rows=8), v("GT"), v("N", 0, P), True, True)
            act(v("SC", rows=8), v("pu", 0, P, rows=8))
            dma("s", hbm(T.ystk), v("out"), "o_stk", DMA + 2600)
            dma("s", hbm(T.ycnt), v("SC", rows=8), "o_cnt", DMA + 2200)
        else:
            pop()
        ts(col("c4", 1), col(m1r, yr0 + cE0 + 1), col(m1s, ys0 + cE0 + 1), Op.max, -1.0, Op.mult, ext=got1)
        act(v("NF"), v(m1r, ur0, ur0 + 16), Fn.Identity, bias=1056.0, ext=got1)
        act(v("nt"), v("JT"), Fn.Identity, bias=col("c4", 1))
        tt(v("uq"), v("nt"), v("dj"), Op.max)
        tt(v("up"), v("uq"), v("NF"), Op.min)
        ts(v("JG"), v(m1r, ur0, ur0 + 16), 1056.0, Op.add, ext=got1)
        if last:
            act(v("XO", 0, V), v("X", 0, V), Fn.Identity, bias=-1024.0, scale=-1024.0)
            tt(v("OG"), ind(v("XF"), v("JG")), v(m2r), Op.max, ext=got2)
        else:
            act(v("OG"), ind(v("XF"), v("JG")))
        tt(v("oj"), v(m3r), v("up"), Op.min, ext=got3)
        cp(v("JU"), v("oj"))
        for c in range(8):
            ju = v("JU", 2 * c, 2 * c + 2)
            if last:
                ts(ind(v("XG"), ju), v("OG", 32 * c, 32 * c + 32), -1024.0, Op.mult, -1024.0, Op.add)
            else:
                tt(ind(v("XF"), ju), v("OG", 32 * c, 32 * c + 32), v(m2r, 32 * c, 32 * c + 32), Op.max, ext=got2)
    dma("s", hbm(T.ylab), v("XO", 0, V), "o_lab", DMA + 2000)

    emit(g, T, ops, sender)
    g.wait_ge(T.sem.sent, sent[0])
    for s in ("o_stk", "o_cnt", "o_lab"):
        g.sync.wait_ge(T.sem[s], 16)


def choose(ops, deps):
    n = len(ops)
    qs = [o[0] for o in ops]
    nm = len(CYC)
    dur = [[float(o[6][m]) for o in ops] for m in range(nm)]
    lat = [[float(o[7][m]) for o in ops] for m in range(nm)]
    covered = [0] * n
    near = []
    for j in range(n):
        mask = 0
        keep = []
        for k in sorted(deps[j], reverse=True):
            if not (mask >> k) & 1 or ops[k][4] is not None:
                keep.append((k, deps[j][k]))
            if deps[j][k]:
                mask |= covered[k]
        near.append(keep)
        for k in deps[j]:
            mask |= covered[k] | (1 << k)
        covered[j] = mask
    after = [[] for _ in range(n)]
    for j in range(n):
        for k, hard in near[j]:
            after[k].append((j, hard))
    gaps = [[[(k, lat[m][k] if hard else 0.0) for k, hard in near[j]] for j in range(n)] for m in range(nm)]
    outs = [[[(k, lat[m][j] if hard else 0.0) for k, hard in after[j]] for j in range(n)] for m in range(nm)]
    pre = [set(k for k, hard in near[j]) for j in range(n)]
    suc = [set(k for k, hard in after[j]) for j in range(n)]
    final = [j for j in range(n) if not after[j]]

    def span(order, m):
        free = {}
        end = [0.0] * n
        for j in order:
            t0 = free.get(qs[j], 0.0)
            for k, x in gaps[m][j]:
                t0 = max(t0, end[k] + x)
            end[j] = free[qs[j]] = t0 + dur[m][j]
        return max(end[j] + lat[m][j] for j in final)

    def schedule(m):
        way = [0.0] * n
        for j in range(n - 1, -1, -1):
            way[j] = dur[m][j] + max([lat[m][j]] + [x + way[k] for k, x in outs[m][j]])
        left = [len(d) for d in near]
        ready = [j for j in range(n) if left[j] == 0]
        early = [0.0] * n
        free = {q: 0.0 for q in "vapgsd"}
        order = []
        while ready:
            t0, first = min((max(early[j], free[qs[j]]), j) for j in ready)
            q = qs[first]
            j = -max((way[k], -k) for k in ready if qs[k] == q and early[k] <= t0 + SLACK)[1]
            free[q] = max(early[j], free[q]) + dur[m][j]
            ready.remove(j)
            order.append(j)
            for k, x in outs[m][j]:
                early[k] = max(early[k], free[q] + x)
                left[k] -= 1
                if left[k] == 0:
                    ready.append(k)
        return order

    def pack(order, m, back):
        du = dur[m]
        start = [0.0] * n
        busy = {q: ([], []) for q in "vapgsd"}
        for j in order:
            t0 = lat[m][j] if back else 0.0
            for k, x in (outs if back else gaps)[m][j]:
                t0 = max(t0, start[k] + du[k] + x)
            a, b = busy[qs[j]]
            lo, hi = 0, len(b)
            while lo < hi:
                mid = (lo + hi) // 2
                if b[mid] > t0:
                    hi = mid
                else:
                    lo = mid + 1
            while lo < len(a) and a[lo] < t0 + du[j]:
                t0 = max(t0, b[lo])
                lo += 1
            a.insert(lo, t0)
            b.insert(lo, t0 + du[j])
            start[j] = t0
        return sorted(range(n), key=lambda j: -start[j] - du[j]), sorted(range(n), key=lambda j: start[j])

    rng = np.random.default_rng(SEED)
    best = schedule(0)
    norm = [span(best, m) / WEIGHT[m] for m in range(nm)]
    score = float(sum(WEIGHT))
    for m in range(nm):
        order = schedule(m)
        for turn in range(TURNS):
            order = pack(pack(pack(order, m, False)[0], m, True)[0], m, False)[1]
            s = sum(span(order, x) / norm[x] for x in range(nm))
            if s < score:
                best, score = order, s

    order = best[:]
    banned = {}
    since = 0
    for it in range(MOVES):
        place = [0] * n
        line = {q: [] for q in "vapgsd"}
        at = [0] * n
        for i, j in enumerate(order):
            place[j] = i
            at[j] = len(line[qs[j]])
            line[qs[j]].append(j)
        before, behind = [n] * n, [n] * n
        for l in line.values():
            for a, b in zip(l[:-1], l[1:]):
                before[b], behind[a] = a, b
        ready, end, rest, tail, whole = [], [], [], [], []
        for m in range(nm):
            du, ga, ou, la = dur[m], gaps[m], outs[m], lat[m]
            r, e, s, t = [0.0] * n, [0.0] * (n + 1), [0.0] * n, [0.0] * (n + 1)
            for j in order:
                t0 = 0.0
                for k, x in ga[j]:
                    if e[k] + x > t0:
                        t0 = e[k] + x
                r[j] = t0
                e[j] = (t0 if t0 > e[before[j]] else e[before[j]]) + du[j]
            for j in reversed(order):
                t0 = la[j]
                for k, x in ou[j]:
                    if t[k] + x > t0:
                        t0 = t[k] + x
                s[j] = t0
                t[j] = (t0 if t0 > t[behind[j]] else t[behind[j]]) + du[j]
            ready.append(r)
            end.append(e)
            rest.append(s)
            tail.append(t)
            whole.append(max(e[j] + la[j] for j in final))
        now = sum(whole[m] / norm[m] for m in range(nm))
        if now < score - 1e-9:
            best, score, since = order[:], now, it
        elif it - since > PATIENCE:
            order, since, banned = best[:], it, {}
            continue
        m0 = it % nm
        e, t = end[m0], tail[m0]
        pairs = [(before[j], j) for j in range(n) if before[j] < n and e[before[j]] + t[j] > whole[m0] - 0.5
                 and ready[m0][j] < e[before[j]] - 0.5]
        tried = []
        for x in rng.permutation(len(pairs))[:WIDTH].tolist():
            a, b = pairs[x]
            l = line[qs[a]]
            far = int(rng.geometric(0.3)) - 1
            for early in (True, False):
                i0, i1 = (max(at[a] - far, 0), at[b]) if early else (at[a], min(at[b] + far, len(l) - 1))
                seg = l[i0:i1 + 1]
                one = seg[-1] if early else seg[0]
                if banned.get(one, -1) > it:
                    continue
                seg = [one] + seg[:-1] if early else seg[1:] + [one]
                guess = 0.0
                for m in range(nm):
                    du, r, s = dur[m], ready[m], rest[m]
                    t0 = end[m][before[l[i0]]]
                    heads = []
                    for j in seg:
                        t0 = t0 if t0 > r[j] else r[j]
                        heads.append(t0)
                        t0 += du[j]
                    t0 = tail[m][behind[l[i1]]]
                    worst, was = 0.0, 0.0
                    for j, h in zip(seg[::-1], heads[::-1]):
                        t0 = (t0 if t0 > s[j] else s[j]) + du[j]
                        worst = max(worst, h + t0)
                        was = max(was, end[m][j] - du[j] + tail[m][j])
                    guess += (worst if was > whole[m] - 0.5 else max(worst, whole[m])) / norm[m]
                tried.append((guess, i0, i1, early, qs[a]))
        tried.sort()
        for guess, i0, i1, early, q in tried:
            a, b = line[q][i0], line[q][i1]
            part = order[place[a]:place[b] + 1]
            one, other, links, beside = (b, a, pre, before) if early else (a, b, suc, behind)
            took, want = [one], set(links[one])
            for k in (part[-2::-1] if early else part[1:]):
                if k in want:
                    if qs[k] == q:
                        break
                    took.append(k)
                    want |= links[k]
                    want.add(beside[k])
            else:
                moved = set(took)
                stay = [k for k in part if k not in moved]
                order[place[a]:place[b] + 1] = took[::-1] + stay if early else stay + took
                banned[one] = it + 5 + int(rng.integers(0, 10))
                banned[other] = it + 3
                break
    return best


def emit(g, T, ops, sender):
    n = len(ops)
    log = {}
    deps = []
    for j, (q, call, rd, wr, sem, ext, dur, lat) in enumerate(ops):
        d = {}
        for acc, w in [(x, False) for x in rd] + [(x, True) for x in wr]:
            name, a, b, st = acc
            ps = SCRATCH[name][0] == "psum"
            lo, hi = (a // 512 * 512, (b + 511) // 512 * 512) if ps else (a, b)
            for (k, l2, h2, w2, a2, b2, st2) in log.get(name, []):
                if l2 >= hi or lo >= h2 or k == j:
                    continue
                if not ps and st * st2 > 1 and not set(range(a, b, st)) & set(range(a2, b2, st2)):
                    continue
                if ops[k][0] != q or ops[k][4] is not None or sem is not None:
                    if w or w2 or ps:
                        d[k] = True
                elif q == "p":
                    if ps:
                        d[k] = False
                elif a2 < b and a < b2 and (w or w2):
                    d[k] = True
            log.setdefault(name, []).append((j, lo, hi, w, a, b, st))
        for s, c in ext:
            d[sender[s]] = True
        if q == "d":
            d[j - 1] = True
        if j in (2, 3, 4, 5):
            d[0 if j == 2 else j - 1] = None
        deps.append(d)
    if not ORDER:
        ORDER.extend(choose(ops, deps))
    order = [j for j in ORDER if ops[j][0] != "d"]
    place = {j: i for i, j in enumerate(ORDER)}
    assert len(ORDER) == n and all(place[k] < place[j] for j in range(n) for k in deps[j])
    queues = {"v": g.vector, "a": g.scalar, "p": g.tensor, "g": g, "s": g.sync}
    counter = {"v": "cv", "a": "ca", "p": "cp", "g": "cg"}
    seen = {}
    need = set()
    waits = {}
    for j in order:
        q = ops[j][0]
        mine = []
        best = {}
        for k, hard in deps[j].items():
            if ops[k][4] is not None:
                if hard and ops[k][4] != "sent" and (q, ops[k][4]) not in seen:
                    seen[(q, ops[k][4])] = 16
                    mine.append((False, ops[k][4], 16))
            elif hard and place[k] > place.get(best.get(ops[k][0]), -1):
                best[ops[k][0]] = k
        for q2, k in best.items():
            if seen.get((q, q2), -1) < place[k]:
                seen[(q, q2)] = place[k]
                need.add(k)
                mine.append((True, q2, k))
        for s, c in ops[j][5]:
            if (q, s) not in seen:
                seen[(q, s)] = c
                mine.append((False, s, c))
        waits[j] = mine
    count = {}
    total = {"v": 0, "a": 0, "p": 0, "g": 0}
    for j in order:
        q, call, sem = ops[j][0], ops[j][1], ops[j][4]
        for own, s, c in waits[j]:
            if own:
                queues[q].wait_ge(T.sem[counter[s]], count[c])
            else:
                queues[q].wait_ge(T.sem[s], c)
        ins = call()
        if sem is not None:
            if sem != "sent":
                ins.then_inc(T.sem[sem], 16)
        elif j in need:
            total[q] += 1
            count[j] = total[q]
            ins.then_inc(T.sem[counter[q]], 1)
